import numpy as np, ml_dtypes
CORES = [40,64,80,88,96,104,120,144]
N = 8
BF = ml_dtypes.bfloat16
def gentries(a):
    return np.ascontiguousarray(a.reshape(8, 16, -1).transpose(0, 2, 1)).reshape(8, -1)
def gtable(e):
    e = np.asarray(e); return np.ascontiguousarray(e.reshape(8, -1, 16).transpose(0, 2, 1)).reshape(128, -1).astype(np.int32)
V, R, K, S, RO = 3072, 3072, 512, 5, 3
def take(a, j):
    return np.take_along_axis(a, j, 2)
def parts(rng, x):
    rec = rng.integers(0, R, (N, 8, V)); pri = take(np.sum(x, axis=2), rec); m = V - 1; q = np.arange(m)
    o = 1 + np.argsort(-pri[..., 1:], axis=2, kind="stable"); ch = []
    for side in range(2):
        u = rng.random((N, 8, m)); p = np.minimum(q + 1 + ((m - 1 - q) * u * u * u).astype(np.int64), m - 1)
        k = np.where((rng.random((N, 8, m)) < 0.1) | (q == m - 1), 0, take(o, p))
        a = rng.integers(0, V, (N, 8, V)); np.put_along_axis(a, o, k, 2); ch.append(a)
    u = rng.random((N, 8, K)); rt = np.where(rng.random((N, 8, K)) < 0.03, 0, take(o, (m * u * u).astype(np.int64)))
    return rec, ch[0], ch[1], rt, rng.integers(0, 256, (N, 8, 16))
def people(rng):
    big = rng.random((N, 8, 16, K)) < 0.35
    return np.where(rng.random((N, 8, 1, K)) < 0.5, rng.integers(0, 16, big.shape), np.where(big, rng.integers(12, 16, big.shape), rng.integers(0, 7, big.shape)))
def pack(x, y, rec, lc, rc, rt, w):
    return {"x": np.ascontiguousarray(x).reshape(N, 128, R).astype(BF), "nw": np.ascontiguousarray(y).reshape(N, 128, K).astype(BF),
            "rec": rec.astype(np.int32), "lc": lc.astype(np.int32), "rc": rc.astype(np.int32), "rt": np.stack([gtable(a) for a in rt]),
            "wt": np.ascontiguousarray(w).reshape(N, 128, 1).astype(np.int32)}
def setup_inputs(rng):
    x = rng.integers(0, 16, (N, 8, 16, R))
    return pack(x, people(rng), *parts(rng, x))
def setup_inputs_ties(rng):
    c = [[8] * 8 + [7, 7, 6, 6, 6, 6, 5, 5], [8] * 8 + [7, 7, 6, 6, 6, 5, 5, 5], [9] + [8] * 7 + [7, 7, 6, 6, 6, 6, 5, 5],
         [8] * 9 + [6, 6, 6, 6, 6, 5, 5], [8] * 9 + [6, 6, 6, 6, 5, 5, 5], [9] + [8] * 8 + [6, 6, 6, 6, 6, 5, 5]]
    a = np.array(c)[rng.integers(0, 6, (N, 8, R))]
    x = np.take_along_axis(a, np.argsort(rng.random(a.shape), axis=3), 3).transpose(0, 1, 3, 2)
    u = rng.random((N, 8, 1, R)); x = np.where(u < 0.06, 0, np.where(u > 0.94, np.where(rng.random(x.shape) < 0.2, 14, 15), x))
    rec, lc, rc, rt, w = parts(rng, x)
    lc = rng.integers(0, V, lc.shape); rc = rng.integers(0, V, rc.shape)
    u = rng.random((N, 8, 1, K)); y = np.where(u < 0.6, 7, people(rng))
    return pack(x, np.where(u > 0.9, np.where(rng.random(y.shape) < 0.15, 14, 15), y), rec, lc, rc, rt, w)
def setup_inputs_ends(rng):
    x = rng.integers(0, 16, (N, 8, 16, R)); rec, lc, rc, rt, w = parts(rng, x)
    lc = np.where(rng.random(lc.shape) < 0.4, 0, lc); rc = np.where(rng.random(rc.shape) < 0.4, 0, rc)
    e = np.array([0, 1, V - 1])
    lc[:, 1] = rng.choice(e, (N, V)); rc[:, 1] = rng.choice(e, (N, V)); rt[:, 1] = rng.choice(e, (N, K))
    rec[:, 2] = rng.choice(np.array([0, R - 1]), (N, V)); rt[:, 3] = rng.choice(e, (N, K))
    rec[:, 4:, 1] = R - 1; rec[:, 4:, V - 1] = 0; rt[:, 5, 0] = V - 1; rt[:, 5, K - 1] = 1
    for q in range(N): rt[q, (q + int(rng.integers(0, 2))) % 8] = 0
    return pack(x, people(rng), rec, lc, rc, rt, w)
def setup_inputs_long(rng):
    x = rng.integers(0, 16, (N, 8, 16, R)); y = people(rng); half = R // 2
    x[:, 0] = rng.integers(1, 16, (N, 16, R)); y[:, 0] = 0
    y[:, 1] = 15; x[:, 1, :, ::16] = 15
    x[:, 2] = rng.integers(9, 16, (N, 16, R)); y[:, 2, :9] = 15; y[:, 2, 9:] = 0
    x[:, 3, 7:] = rng.integers(1, 4, (N, 9, R)); y[:, 3, 7:] = 0; y[:, 3, :7] = 15
    for g in range(4, 8):
        x[:, g, :, :half] = rng.integers(9, 16, (N, 16, half)); x[:, g, :, half:] = rng.integers(0, 7, (N, 16, R - half))
        y[:, g] = np.where(rng.random((N, 1, K)) < 0.5, rng.integers(7, 9, (N, 16, K)), np.where(np.arange(16)[:, None] < 9, 15, 0))
    rec, lc, rc, rt, w = parts(rng, x); out = []
    for a in (lc, rc, rt): out.append(np.where(a == 0, rng.integers(1, V, a.shape), a))
    for g in range(4, 8):
        h = min(g - 3, S - 1); m = V // (h + 1); lev = np.arange(V) % (h + 1)
        for k in range(2): out[k][:, g] = np.where(lev < h, (h + 1) * rng.integers(0, m, (N, V)) + lev + 1, out[k][:, g])
        out[2][:, g] = (h + 1) * rng.integers(1, m, (N, K))
        rec[:, g] = rng.integers(0, half, (N, V)) + np.where(lev == h, half, 0)
    return pack(x, y, rec, out[0], out[1], out[2], w)
def setup_inputs_alike(rng):
    x = rng.integers(0, 16, (N, 8, 16, R)); rec, lc, rc, rt, w = parts(rng, x); y = people(rng); v = np.arange(V)
    rt[:, 0] = rng.integers(1, V, (N, 1)); rt[:, 2] = rng.choice(np.array([1, V - 1, 5]), (N, K))
    rec[:, 1] = rng.integers(0, R, (N, 1)); rec[:, 3] = rng.choice(np.array([0, R - 1, 17]), (N, V))
    lc[:, 4] = np.where(rng.random((N, V)) < 0.5, v, lc[:, 4]); rc[:, 5] = np.where(rng.random((N, V)) < 0.5, v, rc[:, 5]); rc[:, 6] = lc[:, 6]
    y[:, 7] = y[:, 7, :, :1]; y[:, 2, :, ::2] = y[:, 2, :, :1]
    w[0] = 0; w[1] = 255; w[2:] = 0; w[2:, :, int(rng.integers(0, 16))] = rng.integers(1, 256, (N - 2, 8))
    q = K // 4; rt[0, 3, :q] = 0
    y[0, 3, :, :q] = np.where((rng.random((16, q)) < 0.25) & (np.arange(q) % 2 == 1), 14, 15)
    return pack(x, y, rec, lc, rc, rt, w)
def setup_inputs_spread(rng):
    x = (16 * rng.random((N, 8, 16, R)) ** np.exp2(rng.integers(-2, 3, (N, 8, 1, R)))).astype(np.int64)
    y = (16 * rng.random((N, 8, 16, K)) ** np.exp2(rng.integers(-2, 3, (N, 8, 1, K)))).astype(np.int64)
    rec, lc, rc, rt, w = parts(rng, np.minimum(x, 15))
    return pack(np.minimum(x, 15), np.minimum(y, 15), rec, lc, rc, rt, np.minimum((256 * rng.random((N, 8, 16)) ** 4).astype(np.int64), 255))
def check_inputs(d):
    bad = []
    for k in ("x", "nw"):
        a = np.asarray(d[k]).astype(np.float32)
        if not bool(np.all((a >= 0) & (a <= 15) & (a == np.floor(a)))): bad.append("whole numbers and range of " + k)
    for k, hi in (("rec", R - 1), ("lc", V - 1), ("rc", V - 1), ("rt", V - 1), ("wt", 255)):
        if np.min(d[k]) < 0 or np.max(d[k]) > hi: bad.append("range of " + k)
    return bad
def reference(x, nw, rec, lc, rc, rt, wt):
    nodes = V + RO * (S + 1) * K; lane = np.zeros((N, 8, K), np.int64) + np.arange(K)
    xs = np.zeros((N, 8, 16, R + RO * K), np.int64); xs[..., :R] = x.astype(np.float32).astype(np.int64).reshape(N, 8, 16, R)
    y = nw.astype(np.float32).astype(np.int64).reshape(N, 8, 16, K); w = wt.astype(np.int64).reshape(N, 8, 16, 1)
    of = np.zeros((N, 8, nodes), np.int64); of[..., :V] = rec
    pt = np.zeros((N, 8, 2 * nodes + 2 * K), np.int64); pt[..., 0:2 * V:2] = lc; pt[..., 1:2 * V:2] = rc
    def put(m, at, v):
        np.put_along_axis(pt, np.where(m, at, 2 * nodes + K + lane), v, 2)
    c = np.stack([gentries(a) for a in rt]).astype(np.int64)
    for t in range(RO):
        b = V + t * (S + 1) * K; new = b + S * K + lane
        xs[..., R + t * K:R + (t + 1) * K] = y; of[..., b + S * K:b + (S + 1) * K] = R + t * K + lane
        py = np.sum(y, axis=2); hung = lane < 0; went = lane < 0; last = lane * 0
        hole = 2 * nodes + lane; lh = lane * 0; rh = lane * 0; opened = lane * 0
        for s in range(S):
            live = c > 0; n = b + s * K + lane; rn = take(of, c); xc = np.take_along_axis(xs, rn[:, :, None, :], 3)
            hang = live & ~hung & (np.sum(xc, axis=2) < py)
            put(hang, hole, new); lh = np.where(hang, 2 * new, lh); rh = np.where(hang, 2 * new + 1, rh); hung = hung | hang
            high = np.sum(xc > y, axis=2) >= 9
            l = take(pt, 2 * c); r = take(pt, 2 * c + 1)
            of[..., b + s * K:b + (s + 1) * K] = np.where(live, rn, 0); put(live, 2 * n, l); put(live, 2 * n + 1, r)
            put(live, np.where(hung, np.where(high, rh, lh), hole), n)
            opened = np.where(live, np.where(high, 2 * n, 2 * n + 1), opened)
            hole = np.where(live & ~hung, opened, hole)
            lh = np.where(live & hung & ~high, opened, lh); rh = np.where(live & hung & high, opened, rh)
            last = np.where(live, rn, last); went = went | live
            c = np.where(live, np.where(high, l, r), 0)
        xc = np.take_along_axis(xs, take(of, c)[:, :, None, :], 3); high = np.sum(xc > y, axis=2) >= 9
        put(~hung, hole, new); put(~hung & (c > 0), np.where(high, 2 * new + 1, 2 * new), c)
        put(hung, lh, 0); put(hung, rh, 0); put(hung, opened, c)
        made = np.array(pt[..., 2 * nodes:2 * nodes + K])
        if t < RO - 1:
            xl = np.where(went[:, :, None, :], np.take_along_axis(xs, last[:, :, None, :], 3), 0)
            y = np.roll((y + xl + t) & 15, 1, axis=0)
            c = take(made, np.sum(w * y, axis=2) & (K - 1))
    return {"yl": pt[..., 2 * V:2 * nodes:2].astype(np.float32), "yr": pt[..., 2 * V + 1:2 * nodes:2].astype(np.float32), "yt": made.astype(np.float32)}

@@ -1,0 +1,543 @@
+from concourse.bass import DstId, RemoteDMATransfer
+from concourse.mybir import AluOpType as Op, ActivationFunctionType as Act
+
+BF, F32, I32, U16 = "bfloat16", "float32", "int32", "uint16"
+NV, K = 3072, 512
+TB = 16640.0
+XV = 96
+SB = {
+    BF: {"XR": [NV], "X": [9216 + 3072], "B": [9216], "TT": [1152], "TC": [6, 6, 16], "UC": [6, 6, 8], "FC": [6, 192],
+         "ONE": [8, 16], "ID": [8, 16], "W1": [8, 4], "WA": [8, 4], "WN": [8, 4], "WB": [10, 8], "WC": [12, 4], "WQ": [144],
+         "W2": [2, 8], "I12": [8, 12], "SH": [8, 16], "SL": [8, 16], "ZC": [2, 36, 4], "ZI": [3, 36, 4], "ZR": [2, 36, 4],
+         "GG": [8, 16], "F": [8, 96], "FA": [8, 64], "E4": [2, 32], "Q4": [2, 32], "C5": [8, 16], "U0": [8, 16], "L0": [8, 4]},
+    F32: {"OUT": [K], "OUTR": [K], "LAM": [6, 6], "RF": [6, 2, 16], "RT": [192], "THR": [8, 16], "TD": [2, 32], "X4": [8, 4],
+          "TH4": [8, 16], "TH5": [8, 16]},
+    I32: {"RC": [2, 96], "LR": [2, 192], "RTI": [32], "WTI": [4], "UI": [32], "UJ": [32], "PI": [8], "PJ": [8]},
+    U16: {"OF0": [192], "OFA": [32], "OFB": [32], "OFI": [32], "OFR": [32]},
+}
+SB[BF].update({k: [K] for k in ("XA", "BA", "A", "BT", "ZT", "JLO", "HO", "LO", "HI", "LW")})
+SB[BF].update({k: [32, 16] for k in ("LA0", "LA1", "LB0", "LB1", "AP", "SS", "MM")})
+SB[BF].update({k: [384] for k in ("HH", "CH", "EE", "LS")})
+SB[BF].update({k: [192] for k in ("LT", "HG", "LV", "EA", "ES", "HS", "RM", "RM2")})
+SB[F32].update({k: [8] for k in ("COL", "AH", "AL", "SV", "DH", "DL", "FH", "FL", "VH", "VL", "MH", "ML")})
+SCRATCH = {k: ("sbuf", [128] + sh, d) for d, bufs in SB.items() for k, sh in bufs.items()}
+SCRATCH.update({k: ("psum", [128, 16, 32], F32) for k in ("P1a", "P1b")})
+SCRATCH.update({k: ("psum", [128, K], F32) for k in ("P2", "P3", "PH", "PL", "PO")})
+SCRATCH["PR"] = ("psum", [128, 32, 16], F32)
+NDMA = 44
+MSGS = ["LA0", "LB0", "LA1", "LB1"]
+SEMAPHORES = ["cV", "cS", "cP", "cG", "sent"] + ["ar" + m for m in MSGS] + ["d%d" % i for i in range(NDMA)]
+
+
+def relays_for(src, dst, T, topo):
+    if topo.may_write(src, dst):
+        return []
+    out = {}
+    for c in topo.cores_of(src):
+        if c != src and T.rank_of(c) is None and topo.may_write(c, dst):
+            out.setdefault(topo.die(c), c)
+    return sorted(out.values(), key=lambda c: topo.die(c) != topo.die(src))
+
+
+def bits(engines):
+    m = 0
+    for e in engines:
+        m |= 1 << e
+    return m
+
+
+def relay_program(g, core, T, topo):
+    n = len(T.cores)
+    for r in range(n):
+        src, dst = T.cores[r], T.cores[(r + 1) % n]
+        rl = relays_for(src, dst, T, topo)
+        if core not in rl:
+            continue
+        i, w = rl.index(core), 32 // len(rl)
+        got = len(topo.engines(src, core)) // len(rl)
+        rid, pid = topo.addr(dst, core)
+        for m in MSGS:
+            g.wait_ge(T.sem["ar" + m], got)
+            piece = T[m][:, i * w:(i + 1) * w, :]
+            g.remote_dma(piece, piece, T.sem["ar" + m], T.sem.sent, pid, rid, topo.mask(core, dst))
+        g.wait_ge(T.sem.sent, len(MSGS) * len(topo.engines(core, dst)))
+
+
+def rank_program(g, core, T, topo):
+    rank = T.rank_of(core)
+    if rank is None:
+        relay_program(g, core, T, topo)
+        return
+    n = len(T.cores)
+    nxt, prv = T.cores[(rank + 1) % n], T.cores[(rank - 1) % n]
+    Q = {"V": g.vector, "S": g.scalar, "P": g.tensor, "G": g, "Y": g.sync}
+    cnt = {"V": 0, "S": 0, "P": 0, "G": 0}
+    known = {q: {} for q in Q}
+    wr, rd, bank, total = {}, {}, {}, {}
+    nd = [0]
+
+    def wait(q, toks):
+        need = {}
+        for s, c in toks:
+            if q == "P" and s == "cP":
+                continue
+            if c > known[q].get(s, 0) and c > need.get(s, 0):
+                need[s] = c
+        for s, c in need.items():
+            Q[q].wait_ge(T.sem[s], c)
+            known[q][s] = c
+
+    def deps(q, r, w, pb):
+        toks = [wr[k] for k in list(r) + list(w) if k in wr]
+        for k in w:
+            toks += rd.get(k, [])
+        for b in pb:
+            toks += [t for e, t in bank.get(b, {}).items() if e != q]
+        wait(q, toks)
+
+    def note(q, tok, r, w, pb):
+        for k in r:
+            rd.setdefault(k, []).append(tok)
+        for k in w:
+            wr[k] = tok
+            rd[k] = []
+        for b in pb:
+            bank.setdefault(b, {})[q] = tok
+        total[tok[0]] = tok[1]
+
+    def op(q, fn, r=(), w=(), pb=()):
+        deps(q, r, w, pb)
+        cnt[q] += 1
+        fn().then_inc(T.sem["c" + q], 1)
+        note(q, ("c" + q, cnt[q]), r, w, pb)
+
+    def dma(q, out, in_, r=(), w=()):
+        deps(q, r, w, ())
+        s = "d%d" % nd[0]
+        nd[0] += 1
+        Q[q].dma_start(out, in_).then_inc(T.sem[s], 16)
+        note(q, (s, 16), r, w, ())
+
+    V, S, P = g.vector, g.scalar, g.tensor
+
+    def ts(out, a, s1, o0, s2=None, o1=None, **kw):
+        if o1 is None:
+            op("V", lambda: V.tensor_scalar(out, a, s1, None, o0), **kw)
+        else:
+            op("V", lambda: V.tensor_scalar(out, a, s1, s2, o0, o1), **kw)
+
+    def tt(out, a, b, o, **kw):
+        op("V", lambda: V.tensor_tensor(out, a, b, o), **kw)
+
+    def cp(out, a, **kw):
+        op("V", lambda: V.tensor_copy(out, a), **kw)
+
+    def ms(out, c, **kw):
+        op("V", lambda: V.memset(out, c), **kw)
+
+    def scan(out, d0, d1, init, o0, o1, **kw):
+        op("V", lambda: V.tensor_tensor_scan(out, d0, d1, init, o0, o1), **kw)
+
+    def act(out, a, f=Act.Identity, bias=0.0, scale=1.0, **kw):
+        op("S", lambda: S.activation(out, a, f, bias=bias, scale=scale), **kw)
+
+    def mms(lst, **kw):
+        deps("P", kw.get("r", ()), kw.get("w", ()), kw.get("pb", ()))
+        for a in lst[:-1]:
+            P.matmul(*a)
+        op("P", lambda: P.matmul(*lst[-1]), **kw)
+
+    def iota(out, pat, base, cm=0, flt=True, **kw):
+        if flt:
+            op("G", lambda: g.iota(out, pat, base, cm, allow_small_or_imprecise_dtypes=True), **kw)
+        else:
+            op("G", lambda: g.iota(out, pat, base, cm), **kw)
+
+    def sel(out, a, pat, o, base, cm, **kw):
+        op("G", lambda: g.affine_select(out, a, pat, o, 0.0, base, cm), **kw)
+
+    def ks(name, m):
+        return [name + str(i) for i in range(m)]
+
+    sent = [0]
+
+    def send(m, c0, keys):
+        deps("G", keys, (), ())
+        rl = relays_for(core, nxt, T, topo)
+        if not rl:
+            rid, pid = topo.addr(nxt, core)
+            g.remote_dma(T[m][:], T.X[:, c0:c0 + K], T.sem["ar" + m], T.sem.sent, pid, rid, topo.mask(core, nxt))
+            sent[0] += len(topo.engines(core, nxt))
+            return
+        w, tr = 32 // len(rl), []
+        for i, c in enumerate(rl):
+            e = topo.engines(core, c)
+            h = len(e) // len(rl)
+            rid, pid = topo.addr(c, core)
+            tr.append(RemoteDMATransfer(dst_ids=[DstId(rid=rid, pnc=pid)], dma_engine_mask=bits(e[i * h:(i + 1) * h]), remote_sem=T.sem["ar" + m],
+                                        src=T.X[:, c0 + 16 * i * w:c0 + 16 * (i + 1) * w], dst=T[m][:, i * w:(i + 1) * w, :]))
+            sent[0] += h
+        g.remote_dma_fused(tr, local_sem=T.sem.sent)
+
+    rin = relays_for(prv, core, T, topo)
+    arrive = sum(len(topo.engines(c, core)) for c in rin) if rin else len(topo.engines(prv, core))
+    for m in MSGS:
+        wr[m] = ("ar" + m, arrive)
+        total["ar" + m] = arrive
+
+    X, B, F, GG, HH, CH, ID, ONE, TC, UC = T.X, T.B, T.F, T.GG, T.HH, T.CH, T.ID, T.ONE, T.TC, T.UC
+    BN, B0, WBK, WCK, CHK, HK, OF0 = ks("Bn", 4), ks("Bo", 6), ks("WB", 3), ks("WC", 4), ks("CH", 5), ks("H", 5), ks("OF0", 6)
+
+    dma("S", T.LR[:, 0, :], T.lc[:], w=["LR0"])
+    dma("Y", T.LR[:, 1, :], T.rc[:], w=["LR1"])
+    dma("S", T.RC[:, 0, :], T.rec[0::2, :], w=["RC0"])
+    dma("Y", T.RC[:, 1, :], T.rec[1::2, :], w=["RC1"])
+    dma("Y", T.XR[:], T.x[:], w=["XR"])
+    dma("Y", X[:, NV + 2560:NV + 3072], T.nw[:], w=["Y0"])
+    dma("Y", T.RTI[:], T.rt[:], w=["RTI"])
+    dma("Y", T.WTI[:, 0:1], T.wt[:], w=["WTI"])
+
+    ms(T.ZT[:], 0.0, w=["ZT"])
+    ms(ONE[:], 1.0, w=["ONE"])
+    iota(T.PI[:, 0:1], [[0, 1]], 0, 1, flt=False, w=["PI"])
+    iota(T.SV[:, 0:5], [[-1, 5]], 4, w=["SV"])
+    iota(T.LAM[0:32], [[1, 6], [0, 6]], 0, w=["LAM"])
+    iota(T.FC[:, 5, :], [[1, 192]], -256, w=["FC5"])
+    iota(UC[0:32, :, :, 0:5], [[0, 180]], 0, w=["UC"])
+    iota(TC[0:32, :, :, 14:16], [[0, 36], [-19200, 2]], 19200, w=["TCr"])
+    for s in range(5):
+        iota(UC[0:32, s + 1:6, s + 1:6, s], [[0, (5 - s) * (5 - s)]], 19200, r=["UC"], w=["UC%d" % s])
+    iota(TC[0:32, 1:6, 1:6, 14], [[0, 25]], int(TB), w=["TCr"])
+    for s in range(4):
+        iota(UC[0:32, s + 2:6, s + 2:6, s], [[0, (4 - s) * (4 - s)]], int(TB) + 512 * (s + 1), w=["UC%d" % s])
+    sel(ID[:], ONE[:], [[-1, 128]], Op.is_equal, 0, 1, r=["ONE"], w=["ID"])
+    sel(T.W1[:], ONE[:, :, 0:4], [[-16, 8], [0, 4]], Op.is_ge, 0, 1, r=["ONE"], w=["W1"])
+    sel(T.WB[:, 0:4, :], ONE[:, :, 0:4], [[-16, 8], [-1, 4]], Op.is_equal, 0, 1, r=["ONE"], w=["WB0"])
+    sel(T.WA[:], T.W1[:], [[16, 8], [0, 4]], Op.is_ge, 15, -1, r=["W1"], w=["WA"])
+    sel(T.WB[:, 6:10, :], ONE[:, :, 0:4], [[-1, 4], [-16, 8]], Op.is_equal, -2, 1, r=["ONE"], w=["WB2"])
+    sel(T.W2[:], ONE[:, :, 0:2], [[-1, 2], [-16, 8]], Op.is_equal, 0, 1, r=["ONE"], w=["W2"])
+    for i in range(6):
+        act(B[:, i * K:(i + 1) * K], T.ZT[:], Act.Copy, r=["ZT"], w=["Bz%d" % i])
+    ts(T.PJ[:, 5:6], T.PI[:, 0:1], 15, Op.bitwise_and, r=["PI"], w=["PJ5"])
+    for i in range(5):
+        ts(T.PJ[:, i:i + 1], T.PI[:, 0:1], 4 if i == 0 else i - 1, Op.logical_shift_right, 1, Op.bitwise_and, r=["PI"], w=["PJ%d" % i])
+    ms(T.FH[:, 0:1], 9.0, w=["FH0"])
+    ms(T.FL[:, 0:1], 9.0, w=["FL0"])
+    cp(T.COL[:, 0:1], T.PJ[:, 5:6], r=["PJ5"], w=["COL0"])
+    cp(T.AH[:, 0:5], T.PJ[:, 0:5], r=ks("PJ", 5), w=["AH"])
+    ms(T.THR[:, :, 0:8], -8.5, w=["THR0"])
+    ts(T.COL[:, 1:2], T.COL[:, 0:1], 0.5, Op.is_gt, r=["COL0"], w=["COL1"])
+    ts(T.COL[:, 2:3], T.COL[:, 0:1], 192.0, Op.mult, 256.0, Op.add, r=["COL0"], w=["COL2"])
+    ts(T.AL[:, 0:5], T.AH[:, 0:5], -1.0, Op.mult, 1.0, Op.add, r=["AH"], w=["AL"])
+    tt(T.DH[:, 0:5], T.AH[:, 0:5], T.SV[:, 0:5], Op.mult, r=["AH", "SV"], w=["DH"])
+    ms(T.THR[:, :, 8:16], 8.5, w=["THR1"])
+    tt(T.DL[:, 0:5], T.AL[:, 0:5], T.SV[:, 0:5], Op.mult, r=["AL", "SV"], w=["DL"])
+    ts(T.FC[:, 4, :], T.ZT[:, 0:192], T.COL[:, 2:3], Op.add, r=["ZT", "COL2"], w=["FC4"])
+    scan(T.FH[:, 1:6], T.AL[:, 0:5], T.DH[:, 0:5], 9.0, Op.mult, Op.add, r=["AL", "DH"], w=["FH"])
+    scan(T.FL[:, 1:6], T.AH[:, 0:5], T.DL[:, 0:5], 9.0, Op.mult, Op.add, r=["AH", "DL"], w=["FL"])
+    ts(T.FC[:, 4:6, 0:1], T.FC[:, 4:6, 0:1], T.COL[:, 1:2], Op.mult, r=["COL1"], w=["FC4", "FC5"])
+    ts(T.VH[:, 0:6], T.FH[:, 0:6], 512.0, Op.mult, TB, Op.add, r=["FH", "FH0"], w=["VH"])
+    ts(T.VL[:, 0:6], T.FL[:, 0:6], 512.0, Op.mult, TB, Op.add, r=["FL", "FL0"], w=["VL"])
+    ms(T.ZC[:], 0.0, w=["ZC"])
+    tt(T.MH[:, 0:5], T.VH[:, 0:5], T.AH[:, 0:5], Op.mult, r=["VH", "AH"], w=["MH"])
+    tt(T.ML[:, 0:5], T.VL[:, 0:5], T.AL[:, 0:5], Op.mult, r=["VL", "AL"], w=["ML"])
+    for p in range(6):
+        i = 5 - p
+        ts(TC[0:32, :, p, 10], T.LAM[0:32, :, p], T.FL[0:32, i:i + 1], Op.is_gt, T.VL[0:32, i:i + 1], Op.mult,
+           r=["LAM", "FL", "FL0", "VL"], w=["TCm%d" % (2 * p)])
+        ts(TC[0:32, :, p, 11], T.LAM[0:32, :, p], T.FH[0:32, i:i + 1], Op.is_gt, T.VH[0:32, i:i + 1], Op.mult,
+           r=["LAM", "FH", "FH0", "VH"], w=["TCm%d" % (2 * p + 1)])
+
+    ts(T.LR[:, :, 0:1], T.LR[:, :, 0:1], T.COL[:, 1:2], Op.mult, r=["COL1"], w=["LR0", "LR1"])
+    cp(T.FC[:, 0:4:2, :], T.LR[:], r=["LR0", "LR1"], w=["FC0", "FC2"])
+    tt(T.FC[:, 1:4:2, :], T.LR[:], T.FC[:, 0:4:2, :], Op.subtract, r=["LR0", "LR1", "FC0", "FC2"], w=["FC1", "FC3"])
+    for f in (0, 2, 1, 3, 4, 5):
+        dma("Y", B[f::16, 0:NV], T.FC[:, f, :], r=["FC%d" % f] + ks("Bz", 6), w=["Bo%d" % f])
+    for h in range(2):
+        cp(T.RF[:, :, h, :], T.RC[:, h, :], r=["RC%d" % h], w=["RF%d" % h])
+    ts(T.COL[:, 5:6], T.PI[:, 0:1], 63.5, Op.is_gt, 256.0, Op.mult, r=["PI"], w=["COL5"])
+    op("V", lambda: V.transpose(T.RT[:], T.RF[:]), r=["RF0", "RF1"], w=["RT"])
+    ms(T.WQ[:], 0.0, w=["WQ"])
+    ts(T.COL[:, 3:4], T.COL[:, 5:6], 2560.0, Op.add, r=["COL5"], w=["COL3"])
+    for k in range(6):
+        cp(T.OF0[:, k::6], T.RT[:, 32 * k:32 * k + 32], r=["RT"], w=["OF0%d" % k])
+    for s in range(5):
+        i = 4 - s
+        act(TC[0:32, :, s + 1:6, 2 * s], UC[0:32, :, s + 1:6, s], scale=T.AH[0:32, i:i + 1], r=["UC%d" % s, "AH"], w=["TCu%d" % (2 * s)])
+        act(TC[0:32, :, s + 1:6, 2 * s + 1], UC[0:32, :, s + 1:6, s], scale=T.AL[0:32, i:i + 1], r=["UC%d" % s, "AL"], w=["TCu%d" % (2 * s + 1)])
+    act(X[:, 16 * XV:NV], T.XR[:].indirect(T.OF0[:, XV:192]), Act.Copy, r=["XR"] + OF0, w=["XS"])
+    ts(T.WN[:], T.WA[:], -1.0, Op.mult, r=["WA"], w=["WN"])
+    tt(T.WB[:, 4:6, :], T.W2[:], T.WB[:, 6:8, :], Op.subtract, r=["W2", "WB2"], w=["WB1"])
+    cp(T.WC[:, 0:2, :], T.WA[:, :, 0], r=["WA"], w=["WC0"])
+    cp(T.WC[:, 2:4, :], T.WA[:, :, 0], r=["WA"], w=["WC1"])
+    cp(T.WC[:, 4:12, 2:4], T.WA[:, :, 0:2], r=["WA"], w=["WC2"])
+    cp(T.WC[:, 4:12, 0:2], T.WN[:, :, 0:2], r=["WN"], w=["WC3"])
+    cp(X[:, 0:16 * XV], T.XR[:].indirect(T.OF0[:, 0:XV]), r=["XR"] + OF0, w=["XV"])
+    cp(T.OFA[:], T.RTI[:], r=["RTI"], w=["OFA"])
+    ms(X[:, 0:1], 0.0, w=["XV"])
+    dma("Y", B[:, 3072:6144], B[:, 0:3072], r=B0, w=["Bi0"])
+    dma("Y", B[:, 6144:9216], B[:, 0:3072], r=B0, w=["Bi1"])
+
+    def table_hung(ss):
+        for s in ss:
+            i = 4 - s
+            ts(TC[0:32, :, 0:s + 1, 2 * s], T.LAM[0:32, :, 0:s + 1], T.FH[0:32, i:i + 1], Op.is_gt, T.MH[0:32, i:i + 1], Op.mult,
+               r=["LAM", "FH", "FH0", "MH"], w=["TCh%d" % (2 * s)])
+            ts(TC[0:32, :, 0:s + 1, 2 * s + 1], T.LAM[0:32, :, 0:s + 1], T.FL[0:32, i:i + 1], Op.is_gt, T.ML[0:32, i:i + 1], Op.mult,
+               r=["LAM", "FL", "FL0", "ML"], w=["TCh%d" % (2 * s + 1)])
+
+    def table_alias():
+        cp(TC[0:32, :, 1:6, 12:14], TC[0:32, :, 1:6, 0:2], r=["TCu0", "TCu1"], w=["TCa0"])
+        cp(TC[0:32, :, 0, 12:14], TC[0:32, :, 0, 10:12], r=["TCm0", "TCm1"], w=["TCa1"])
+
+    def table_turn(j):
+        keys = ks("TCh", 10) + ks("TCu", 10) + ks("TCm", 12) + ["TCa0", "TCa1", "TCr"]
+        mms([(T.PO[0:16, 32 * c:32 * c + 32], TC[0:32, 2 * j + c // 6, c % 6, :], ID[0:32, 0:2, :], True, True) for c in range(12)],
+            r=keys + ["ID"], pb=["PO"])
+        act(T.TT[0:16, 384 * j:384 * j + 384], T.PO[0:16, 0:384], Act.Copy, w=["TT%d" % j], pb=["PO"])
+
+    iota(CH[:], [[0, 384]], 0, w=CHK)
+    iota(HH[:], [[0, 384]], 0, w=HK)
+    send("LA0", NV + 2560, ["Y0"])
+    iota(T.ZR[:], [[0, 288]], 0, w=["ZR0", "ZR1"])
+    iota(T.X4[:], [[0, 8], [1, 4]], 0, 4, w=["X4"])
+    iota(T.RM2[:], [[0, 192]], 2, w=["RM2"])
+    iota(T.RM[:], [[0, 192]], 1, w=["RM"])
+    iota(T.ZI[:], [[0, 432]], 0, w=ks("ZI", 3))
+    iota(T.RM2[:, 0::6], [[0, 32]], 0, w=["RM2"])
+    iota(T.RM[:, 0::6], [[0, 32]], 0, w=["RM"])
+    iota(T.JLO[:], [[0, 2], [1, 256]], 0, w=["JLO"])
+    iota(T.FA[:, :, 16:64], [[0, 384]], 0, w=["FAz"])
+    sel(T.I12[:], ONE[:, :, 0:12], [[-16, 8], [-1, 12]], Op.is_equal, 0, 1, r=["ONE"], w=["I12"])
+    iota(T.SH[:, :, 8:16], [[0, 64]], 0, w=["SH0"])
+    iota(T.SL[:, :, 8:16], [[0, 64]], 0, w=["SL0"])
+    sel(T.SH[:, :, 0:8], ONE[:, :, 0:8], [[-16, 8], [-1, 4], [1000, 2]], Op.is_equal, -12, 1, r=["ONE"], w=["SH1"])
+    sel(T.SL[:, :, 0:8], ONE[:, :, 0:8], [[-16, 8], [-1, 4], [1000, 2]], Op.is_equal, -1012, 1, r=["ONE"], w=["SL1"])
+
+    def wrap(Z, parts, pn, c0, keys):
+        lst = [(T[pn][:, c0:c0 + 32], Z[:, p, 3 - e:35 - e, :], ID[:, :, e::4]) for p in parts for e in range(4)]
+        mms([a + (i == 0, i == len(lst) - 1) for i, a in enumerate(lst)], r=keys + ["ID"], pb=[pn])
+
+    PU = T.P3[:, 64:96]
+
+    def weigh(src, rs, keys, first=False, final=False):
+        mms([(PU, T.WQ[:, 15 - r:143 - r], src[:, :, r], first and r == 0, final and r == 15) for r in rs], r=["WQ"] + keys, pb=["P3"])
+
+    offs = ["OFA", "OFB"]
+    cur = [0]
+    ZW = T.ZC[:, :, 3:35:4, :]
+    PN = ["P1a", "P1b"] * 3
+    CN = ["PH", "PL", "PH", "PL", "PH", "P2"]
+    for t in range(3):
+        Bt = NV + 3072 * t
+        last = t == 2
+        yk = "Y%d" % t
+        y = X[:, Bt + 2560:Bt + 3072]
+        xk = ["XV", "XS"] + ["R%d_%d" % (u, s) for u in range(t) for s in range(6)] + ks("Y", t)
+        la, lb = "LA%d" % min(t, 1), "LB%d" % min(t, 1)
+        ap, ak = (T.AP, "AP") if t else (T[la], la)
+
+        def pri(s):
+            lst = []
+            for b in range(4):
+                a, c = Bt + K * s + b, Bt + 2560 + b
+                lst += [(T.PR[:, b::4, s], X[:, a:a + K - b:4], T.WA[:, :, 0], True, False), (T.PR[:, b::4, s], X[:, c:c + K - b:4], T.WN[:, :, 0], False, True)]
+            mms(lst, r=["R%d_%d" % (t, s), yk, "WA", "WN"] + (["R%d_5" % t] if s == 4 else []), pb=["PR"])
+            if s == 0 and not last:
+                lst = []
+                for b in range(4):
+                    a, c = Bt + b, Bt + 2560 + b
+                    o = T.P3[:, 128 + b:256:4]
+                    lst += [(o, X[:, a:a + K - b:4], T.WA[:], True, False), (o, X[:, c:c + K - b:4], T.WN[:], False, True)]
+                mms(lst, r=["R%d_0" % t, yk, "WA", "WN"], pb=["P3"])
+
+        def sides(s, thr, keys):
+            tt(GG[:], T[CN[s]][:, 128:256], thr, Op.is_gt, r=keys, w=["GG"], pb=[CN[s]])
+
+        def kept(s):
+            tt(F[:, :, 16 * s:16 * s + 16], GG[:], T[PN[s]][:, 0:4, :], Op.mult, r=["GG"], w=["F%d" % s], pb=[PN[s]])
+
+        for s in range(6):
+            on = offs[cur[0]]
+            off = T[on]
+            pn, cn = PN[s], CN[s]
+            P1, PC = T[pn], T[cn]
+            if s == 0 and t:
+                xw, xr, bw, bk = T.XA[:], ["XA"], T.BA[:], ["BA"]
+            else:
+                xw, xr, bw, bk = X[:, 0:Bt], xk, B[:, 0:Bt], B0 + (BN if t else [])
+            r0 = Bt + K * s
+            if s == 4:
+                cp(X[:, r0:r0 + 256], xw.indirect(off[:, 0:16]), r=xr + [on], w=["R%d_4" % t])
+                act(X[:, r0 + 256:r0 + K], xw.indirect(off[:, 16:32]), Act.Copy, r=xr + [on], w=["R%d_5" % t])
+                if not last:
+                    send(lb, r0, ["R%d_4" % t, "R%d_5" % t])
+            tt(T.A[:], xw.indirect(off[:]), y, Op.is_gt, r=xr + [on, yk], w=["A"])
+            if s < 5:
+                act(T.BT[:], bw.indirect(off[:]), Act.Copy, r=bk + [on], w=["BT"])
+            if s < 4:
+                act(X[:, r0:r0 + K], xw.indirect(off[:]), Act.Copy, r=xr + [on], w=["R%d_%d" % (t, s)])
+            if s == 4 and not last:
+                act(T.XA[:], X[:, Bt:Bt + 3072].indirect(T.OFR[:]), Act.Copy, r=ks("R%d_" % t, 6) + [yk, "OFR"], w=["XA"])
+            if s == 5:
+                for h in range(2):
+                    act(T.HO[:, 256 * h:256 * h + 256], T.TT[:].indirect(T.OFI[:, 16 * h:16 * h + 16]), Act.Relu,
+                        bias=Bt + 256.0 * h - TB, r=ks("TT", 3) + ks("TR", 8) + ["OFI"], w=["HO%d" % h])
+                for d in range(4):
+                    act(T.TH5[:, :, 4 * d:4 * d + 4], T.EA[:, 4::6], bias=183.5 + 17 * (d // 2), scale=-1.0, r=["EA"], w=["TH5%d" % d])
+                for d in range(4):
+                    act(T.C5[:, :, 4 * d:4 * d + 4], T.ZC[:, d % 2, 3:35:4, :], Act.Copy, r=["ZC"], w=["C5%d" % d])
+                if t == 1:
+                    act(T.AP[:], T[la][:], bias=float(t), r=[la], w=["AP"])
+                if t == 0:
+                    weigh(ap, range(16), [ak], first=True)
+            if t and s < 2:
+                act(T.OUT[0:96, 256 * s:256 * s + 256], T.PO[0:96, 256 * s:256 * s + 256], Act.Copy, w=[("OUT", "OUTb")[s]], pb=["PO"])
+                if s:
+                    dma("Y", T.yl[:, Bt - 2 * NV:Bt - NV], T.OUT[0:96:2, :], r=["OUT", "OUTb"])
+                    dma("Y", T.yr[:, Bt - 2 * NV:Bt - NV], T.OUT[1:96:2, :], r=["OUT", "OUTb"])
+            if 1 <= s <= 4:
+                pri(s - 1)
+            if s == 4:
+                pri(4)
+            if t == 0 and s in (1, 2, 3):
+                table_turn(s - 1)
+                if s == 3:
+                    for q in range(1, 8):
+                        dma("Y", T.TT[16 * q:16 * q + 16, :], T.TT[0:16, :], r=ks("TT", 3), w=["TR%d" % q])
+            mms([(PC[:, 64 + b:256:4], T.A[:, b::4], T.WC[:], True, True) for b in range(4)], r=["A"] + WCK, pb=[cn])
+            if s < 5:
+                nq = 10 if s == 0 else 8
+                mms([(P1[:, 0:nq, b::4], T.BT[:, b::4], T.WB[:, 0:nq, :], True, True) for b in range(4)], r=["BT"] + WBK, pb=[pn])
+
+            if t == 0 and s == 0:
+                table_hung(range(2))
+            if s == 1 and not last:
+                ts(T.U0[:], T.P3[:, 128:256], 0.0, Op.is_ge, w=["U0"], pb=["P3"])
+                a, ka = T.U0[:, :, 0:4], "U0"
+                if t == 0:
+                    ts(T.L0[:], CH[:, 0:192:6], 0.0, Op.is_gt, r=["CH0"], w=["L0"])
+                    ts(T.ZR[:, 1, 3:35:4, :], T.X4[:], T.COL[:, 5:6], Op.subtract, r=["X4", "COL5"], w=["ZR1"])
+                    tt(T.L0[:], T.L0[:], a, Op.mult, r=["U0"], w=["L0"])
+                    a, ka = T.L0[:], "L0"
+                ts(T.ZR[:, 0, 3:35:4, :], a, -2560.0, Op.mult, T.COL[:, 3:4], Op.add, r=[ka, "COL3"], w=["ZR0"])
+            if s == 2 and not last:
+                if t == 0:
+                    cp(T.COL[:, 4:5], T.WTI[:, 0:1], r=["WTI"], w=["COL4"])
+                cp(T.OFR[:], T.P3[:, 32:64], w=["OFR"], pb=["P3"])
+                if t == 0:
+                    ts(T.WQ[:, 15:143:16], T.WA[:, :, 0], T.COL[:, 4:5], Op.mult, r=["WA", "COL4"], w=["WQ"])
+            if s == 3 and not last:
+                scan(T.LS[:], T.EE[:], CH[:], 0.0, Op.mult, Op.add, r=["EE0", "EE1"] + CHK, w=["LS"])
+            if s == 4:
+                ts(T.LT[:], T.PR[:, :, 0:6], 0.0, Op.is_lt, 32.0, Op.mult, r=["PR5"], w=["LT"], pb=["PR"])
+                ts(T.LV[:], CH[:, 0:192], 0.0, Op.is_gt, 192.0, Op.mult, r=CHK, w=["LV"])
+                scan(T.HG[:], T.RM[:], T.LT[:], 0.0, Op.mult, Op.max, r=["RM", "LT"], w=["HG"])
+            if s == 5:
+                tt(T.LO[:], T.HO[:], T.JLO[:], Op.min, r=["HO0", "HO1", "JLO"], w=["LO"])
+                sides(5, T.TH5[:], ks("TH5", 4))
+                if not last:
+                    tt(T.FA[:, :, 0:16], T.U0[:], F[:, :, 0:16], Op.mult, r=["F0", "U0"], w=["FA"])
+                tt(F[:, :, 80:96], GG[:], T.C5[:], Op.mult, r=["GG"] + ks("C5", 4), w=["F5"])
+                break
+
+            ts(HH[:, s::6], PC[:, 64:128], 8.5, Op.is_gt, w=["H%d" % s], pb=[cn])
+            if s < 4:
+                sides(s, T.THR[:], ["THR0", "THR1"])
+            if s == 4:
+                tt(T.EA[:], T.LV[:], T.HG[:], Op.subtract, r=["LV", "HG"], w=["EA"])
+            tt(T.TD[:], HH[:, s::6], P1[:, 4:6, :], Op.mult, r=["H%d" % s], w=["TD"], pb=[pn])
+            if s == 4:
+                ts(T.ZI[:, 2, 3:35:4, :], PC[:, 64:96], 8.5, Op.is_gt, 16.0, Op.mult, w=["ZI2"], pb=[cn])
+            if s == 3 and not last:
+                tt(CH[:, 4::6], T.TD[:], P1[:, 6:8, :], Op.add, r=["TD"], w=["CH4"], pb=[pn])
+                for p in range(2):
+                    ts(T.E4[:, p, :], CH[:, 4:192:6], 0.0, Op.is_equal, r=["CH4"], w=["E4%d" % p])
+                tt(T.Q4[:], T.E4[:], T.LS[:, 3::6], Op.mult, r=["E40", "E41", "LS"], w=["Q4"])
+                tt(ZW, T.Q4[:], CH[:, 4::6], Op.add, r=["Q4", "CH4"], w=["ZC"])
+            else:
+                tt(ZW, T.TD[:], P1[:, 6:8, :], Op.add, r=["TD"], w=["ZC"], pb=[pn])
+            wrap(T.ZC, (0, 1), "P2", 0, ["ZC"])
+            if s == 0:
+                cp(CH[:, 0::6], P1[:, 8:10, :], w=["CH0"], pb=[pn])
+            if s < 4:
+                kept(s)
+            if s < 3 or (last and s == 3):
+                cp(CH[:, s + 1::6], ZW, r=["ZC"], w=["CH%d" % (s + 1)])
+            if t == 0 and s == 0:
+                table_hung(range(2, 5))
+                table_alias()
+                ms(T.PR[:, :, 5], 0.0, w=["PR5"], pb=["PR"])
+            if s == 2 and not last:
+                for p in range(2):
+                    ts(T.EE[:, 192 * p:192 * p + 192], CH[:, 0:192], 0.0, Op.is_equal, r=CHK, w=["EE%d" % p])
+                ms(T.EE[:, 0::6], 0.0, w=["EE0", "EE1"])
+            if s == 3:
+                scan(T.HS[:], T.RM2[:], HH[:, 0:192], 0.0, Op.mult, Op.add, r=["RM2"] + HK, w=["HS"])
+            if s == 4:
+                scan(T.ES[:], T.RM[:], T.EA[:], 0.0, Op.mult, Op.add, r=["RM", "EA"], w=["ES"])
+                cp(T.ZI[:, 0, 3:35:4, :], T.HS[:, 3::6], r=["HS"], w=["ZI0"])
+                ts(T.ZI[:, 1, 3:35:4, :], T.ES[:, 4::6], 160.0, Op.add, r=["ES"], w=["ZI1"])
+                tt(T.X4[:], T.LV[:, 4::6], T.HG[:, 4::6], Op.add, r=["LV", "HG"], w=["X4"])
+                wrap(T.ZI, (2, 0, 1), "P3", 0, ks("ZI", 3))
+                for d in range(4):
+                    act(T.TH4[:, :, 4 * d:4 * d + 4], T.X4[:], bias=183.5 + 17 * (d // 2), scale=-1.0, r=["X4"], w=["TH4%d" % d])
+            cur[0] ^= 1
+            cp(T[offs[cur[0]]][:], T.P2[:, 0:32], w=[offs[cur[0]]], pb=["P2"])
+            if s == 1 and not last:
+                wrap(T.ZR, (0, 1), "P3", 32, ["ZR0", "ZR1"])
+            if s == 4:
+                sides(4, T.TH4[:], ks("TH4", 4))
+                cp(T.OFI[:], T.P3[:, 0:32], w=["OFI"], pb=["P3"])
+                kept(4)
+
+        fk = ks("F", 6) + ["ID"]
+        if last:
+            hv = ((T.PO, 0), (T.PL, 1))
+            mms([(p[0:96, 0:256], T.I12[:], T.HO[:, 256 * h:256 * h + 256], True, False) for p, h in hv] +
+                [(T.PH[0:8, :], ID[:, :, 14], T.HO[:], True, False)], r=["HO0", "HO1", "I12", "ID"], pb=["PO", "PL", "PH"])
+            mms([(p[0:96, 0:256], T.I12[:], T.LO[:, 256 * h:256 * h + 256], False, False) for p, h in hv], r=["LO"], pb=["PO", "PL"])
+            for h, nm in enumerate(("PO", "PL")):
+                mms([(T[nm][0:96, i // 2:256:4], F[:, :, 4 * (i % 2) + i // 2::8], ID[:, 4 * h:4 * h + 4, :], False, i == 7) for i in range(8)],
+                    r=fk, pb=[nm])
+            mms([(T.PH[0:8, :], ID[:, :, 14], T.LO[:], False, True)], r=["LO"], pb=["PH"])
+            act(T.OUT[0:96, 0:256], T.PO[0:96, 0:256], Act.Copy, w=["OUT"], pb=["PO"])
+            cp(T.OUT[0:96, 256:K], T.PL[0:96, 0:256], w=["OUTb"], pb=["PL"])
+            dma("S", T.yl[:, Bt - NV:Bt], T.OUT[0:96:2, :], r=["OUT", "OUTb"])
+            dma("Y", T.yr[:, Bt - NV:Bt], T.OUT[1:96:2, :], r=["OUT", "OUTb"])
+            cp(T.OUTR[0:8, :], T.PH[0:8, :], w=["OUTR"], pb=["PH"])
+            dma("S", T.yt[:], T.OUTR[0:8, :], r=["OUTR"])
+            break
+        mms([(T.PH[0:96, :], T.I12[:], T.HO[:], True, False), (T.PO[:], T.SH[:], T.HO[:], True, False)], r=["HO0", "HO1", "I12", "SH0", "SH1"], pb=["PH", "PO"])
+        mms([(T.PO[:], T.SL[:], T.LO[:], False, False), (T.PL[0:96, :], T.I12[:], T.LO[:], True, False)], r=["LO", "I12", "SL0", "SL1"], pb=["PL", "PO"])
+        mms([(T.PO[:, b::4], T.FA[:, :, b::4], ID[:], False, b == 3) for b in range(4)], r=["FA", "FAz", "ID"], pb=["PO"])
+        act(T.BA[:], T.PO[:], Act.Copy, w=["BA"], pb=["PO"])
+        for nm, part in (("PH", 0), ("PL", 4)):
+            mms([(T[nm][0:96, b::4], F[:, :, part + b::8], ID[:], False, b == 3) for b in range(4)], r=fk, pb=[nm])
+        if t:
+            weigh(ap, range(16), [ak], first=True)
+        act(T.HI[0:96, :], T.PH[0:96, :], Act.Copy, w=["HI"], pb=["PH"])
+        act(T.LW[0:96, :], T.PL[0:96, :], Act.Copy, w=["LW"], pb=["PL"])
+        for part, nm in enumerate(("HI", "LW")):
+            for side in range(2):
+                dma("Y", B[2 * side + part::16, Bt:Bt + 3072], T[nm][side:96:2, :], r=[nm, "Bi%d" % t], w=["Bn%d" % (2 * side + part)])
+
+        weigh(T[lb], range(16), [lb])
+        for h in range(2):
+            c = slice(8 * h, 8 * h + 8)
+            tt(T.SS[:, :, c], ap[:, :, c], T[lb][:, :, c], Op.add, r=[ak, lb], w=["SS%d" % h])
+            ts(T.MM[:, :, c], T.SS[:, :, c], 15.5, Op.is_gt, -16.0, Op.mult, r=["SS%d" % h], w=["MM%d" % h])
+            weigh(T.MM, range(8 * h, 8 * h + 8), ["MM%d" % h], final=True)
+        n0 = Bt + 3072 + 2560
+        tt(X[:, n0:n0 + K], T.SS[:], T.MM[:], Op.add, r=ks("SS", 2) + ks("MM", 2), w=["Y%d" % (t + 1)])
+        if t == 0:
+            send("LA1", n0, ["Y1"])
+        mms([(T.PO[0:96, :], ID[0:96, 0:6, :], T.HI[0:96, :], True, False), (T.PO[0:96, :], ID[0:96, 0:6, :], T.LW[0:96, :], False, True)],
+            r=["ID", "HI", "LW"], pb=["PO"])
+        cp(T.UI[:], PU, w=["UI"], pb=["P3"])
+        ts(T.UJ[:], T.UI[:], K - 1, Op.bitwise_and, r=["UI"], w=["UJ"])
+        cur[0] ^= 1
+        cp(T[offs[cur[0]]][:], T.UJ[:], r=["UJ"], w=[offs[cur[0]]])
+
+    total["sent"] = sent[0]
+    wait("G", list(total.items()))

@@ -4,28 +4,35 @@ from concourse.mybir import AluOpType as Op, ActivationFunctionType as Act
 BF, F32, I32, U16 = "bfloat16", "float32", "int32", "uint16"
 NV, K = 3072, 512
 TB = 16640.0
-XV = 96
+XV = 86
+X4V = 18
+FOLD = (1,)
+LOOK = (0, 2, 2)
+GAPS = ({"0c": "hung", "0w": "WM LV0 ZR1 roots", "1c": "U0 over under root LS1 T0", "1w": "FA base both RM4", "2c": "OFR ID8 ID4 ID2 IDN", "2w": "weight J0", "3c": "LS0 WQ", "3w": "ZI0 ZI1", "3e": "OFD"}, {"0c": "OFC ON ZR1", "0w": "owed0", "1c": "U0 base root T0", "1w": "owed1", "2c": "OFR end", "2w": "FA", "3c": "LS0 J1", "3w": "ZI0 ZI1", "3e": "OFD"}, {"0c": "OFC F2l I12N", "0w": "owed0", "1c": "U0 root T0", "1w": "owed1", "2c": "end", "3w": "ZI0 ZI1"})
+SIDE = ({}, {"0m": "lo0", "1w": "lo1", "1m": "hi0", "2w": "hi1 a0", "2m": "a1", "3w": "b0", "3m": "b1"}, {"0w": "lo0 lo1", "0m": "hi0", "1w": "hi1 out", "1m": "j", "2w": "m0 m1", "2m": "n0", "3w": "n1 k", "3m": "e0", "4w": "e1 e2 e3"})
 SB = {
-    BF: {"XR": [NV], "X": [9216 + 3072], "B": [9216], "TT": [1152], "TC": [6, 6, 16], "UC": [6, 6, 8], "FC": [6, 192],
-         "ONE": [8, 16], "ID": [8, 16], "W1": [8, 4], "WA": [8, 4], "WN": [8, 4], "WB": [10, 8], "WC": [12, 4], "WQ": [144],
-         "W2": [2, 8], "I12": [8, 12], "SH": [8, 16], "SL": [8, 16], "ZC": [2, 36, 4], "ZI": [3, 36, 4], "ZR": [2, 36, 4],
-         "GG": [8, 16], "F": [8, 96], "FA": [8, 64], "E4": [2, 32], "Q4": [2, 32], "C5": [8, 16], "U0": [8, 16], "L0": [8, 4]},
-    F32: {"OUT": [K], "OUTR": [K], "LAM": [6, 6], "RF": [6, 2, 16], "RT": [192], "THR": [8, 16], "TD": [2, 32], "X4": [8, 4],
-          "TH4": [8, 16], "TH5": [8, 16]},
-    I32: {"RC": [2, 96], "LR": [2, 192], "RTI": [32], "WTI": [4], "UI": [32], "UJ": [32], "PI": [8], "PJ": [8]},
-    U16: {"OF0": [192], "OFA": [32], "OFB": [32], "OFI": [32], "OFR": [32]},
+    BF: {"X": [9216 + 3072], "B": [9216 + 1024], "TT": [1152], "TC": [6, 6, 16], "UC": [6, 6, 8], "FC": [4, 192],
+         "WP": [8, 5], "WM": [8], "WQ": [144], "I12": [64, 2], "I12N": [64, 2], "SM": [64, 2],
+         "ZC": [36, 8], "ZR": [36, 8], "ZI": [36, 16], "GG": [5, 8, 16], "G5": [8, 16], "F": [64, 16], "F2": [32, 16],
+         "F5": [32, 16], "U0": [32], "T0": [32], "TMP": [32], "LV": [5, 32]},
+    F32: {"OUT": [K], "OUM": [K], "OUE": [K], "LAM": [12, 6], "A3": [108], "COL": [16], "RF": [6, 2, 16], "RT": [192], "TD": [32, 2], "LN": [8, 4]},
+    I32: {"RC": [2, 96], "LR": [2, 192], "RTI": [32], "WTI": [4], "UI": [32], "UJ": [32], "PI": [8], "PK": [8], "PJ": [36]},
+    U16: {"OF0": [192], "OFA": [32], "OFB": [32], "OFC": [32], "OFD": [32], "OFI": [32], "OFR": [32]},
 }
-SB[BF].update({k: [K] for k in ("XA", "BA", "A", "BT", "ZT", "JLO", "HO", "LO", "HI", "LW")})
-SB[BF].update({k: [32, 16] for k in ("LA0", "LA1", "LB0", "LB1", "AP", "SS", "MM")})
-SB[BF].update({k: [384] for k in ("HH", "CH", "EE", "LS")})
-SB[BF].update({k: [192] for k in ("LT", "HG", "LV", "EA", "ES", "HS", "RM", "RM2")})
-SB[F32].update({k: [8] for k in ("COL", "AH", "AL", "SV", "DH", "DL", "FH", "FL", "VH", "VL", "MH", "ML")})
+SB[BF].update({k: [K] for k in ("XA", "A", "A5", "BT", "ZT", "J0", "J1", "ON", "HO", "LO", "E1", "E2")})
+SB[BF].update({k: [32, 16] for k in ("LA0", "LA1", "LB0", "LB1", "SS", "MM")})
+SB[BF].update({k: [8, 16] for k in ("ONE", "ID", "IDM", "IDP", "IDN", "ID2", "ID4", "ID8", "SA", "SB")})
+SB[BF].update({k: [8, 12] for k in ("SE0", "SE1", "SE2")})
+SB[BF].update({k: [8, 8] for k in ("SG", "WC", "WB", "WR")})
+SB[BF].update({k: [32, 2] for k in ("H4", "N4", "Q4", "Q5", "CM", "CH", "E4", "LS")})
+SB[BF].update({k: [128] for k in ("LT", "W4", "RM4", "NH")})
+SB[F32].update({k: [72] for k in ("SV", "DD", "FF", "MK", "VV", "MX")})
 SCRATCH = {k: ("sbuf", [128] + sh, d) for d, bufs in SB.items() for k, sh in bufs.items()}
-SCRATCH.update({k: ("psum", [128, 16, 32], F32) for k in ("P1a", "P1b")})
-SCRATCH.update({k: ("psum", [128, K], F32) for k in ("P2", "P3", "PH", "PL", "PO")})
+SCRATCH.update({k: ("psum", [128, 16, 4, 8], F32) for k in ("P1", "PC0", "PC1", "PO", "PL")})
+SCRATCH.update({k: ("psum", [128, K], F32) for k in ("PW", "PX")})
 SCRATCH["PR"] = ("psum", [128, 32, 16], F32)
-NDMA = 44
-MSGS = ["LA0", "LB0", "LA1", "LB1"]
+NDMA = 58
+MSGS = [m + str(t) for t in range(2) for m in ("LA", "LB") if m == "LB" or t not in FOLD]
 SEMAPHORES = ["cV", "cS", "cP", "cG", "sent"] + ["ar" + m for m in MSGS] + ["d%d" % i for i in range(NDMA)]
 
 
@@ -111,11 +118,14 @@ def rank_program(g, core, T, topo):
         fn().then_inc(T.sem["c" + q], 1)
         note(q, ("c" + q, cnt[q]), r, w, pb)
 
-    def dma(q, out, in_, r=(), w=()):
+    def dma(q, out, in_, r=(), w=(), add=False):
         deps(q, r, w, ())
         s = "d%d" % nd[0]
         nd[0] += 1
-        Q[q].dma_start(out, in_).then_inc(T.sem[s], 16)
+        if add:
+            Q[q].dma_start(out, in_, accum_op=Op.add, max_dma_last_dim=2048).then_inc(T.sem[s], 16)
+        else:
+            Q[q].dma_start(out, in_).then_inc(T.sem[s], 16)
         note(q, (s, 16), r, w, ())
 
     V, S, P = g.vector, g.scalar, g.tensor
@@ -153,29 +163,25 @@ def rank_program(g, core, T, topo):
         else:
             op("G", lambda: g.iota(out, pat, base, cm), **kw)
 
-    def sel(out, a, pat, o, base, cm, **kw):
-        op("G", lambda: g.affine_select(out, a, pat, o, 0.0, base, cm), **kw)
+    def sel(out, a, pat, o, base, cm, fill=0.0, **kw):
+        op("G", lambda: g.affine_select(out, a, pat, o, fill, base, cm), **kw)
 
     def ks(name, m):
         return [name + str(i) for i in range(m)]
 
     sent = [0]
 
-    def send(m, c0, keys):
+    def send(m, srcs, keys):
         deps("G", keys, (), ())
-        rl = relays_for(core, nxt, T, topo)
-        if not rl:
-            rid, pid = topo.addr(nxt, core)
-            g.remote_dma(T[m][:], T.X[:, c0:c0 + K], T.sem["ar" + m], T.sem.sent, pid, rid, topo.mask(core, nxt))
-            sent[0] += len(topo.engines(core, nxt))
-            return
+        rl = relays_for(core, nxt, T, topo) or [nxt]
         w, tr = 32 // len(rl), []
         for i, c in enumerate(rl):
             e = topo.engines(core, c)
             h = len(e) // len(rl)
             rid, pid = topo.addr(c, core)
+            pieces = [a[:, c0 + 16 * i * w:c0 + 16 * (i + 1) * w] for a, c0 in srcs]
             tr.append(RemoteDMATransfer(dst_ids=[DstId(rid=rid, pnc=pid)], dma_engine_mask=bits(e[i * h:(i + 1) * h]), remote_sem=T.sem["ar" + m],
-                                        src=T.X[:, c0 + 16 * i * w:c0 + 16 * (i + 1) * w], dst=T[m][:, i * w:(i + 1) * w, :]))
+                                        srcs=pieces, dsts=[T[m][:, i * w:(i + 1) * w, :]], alu_op=1 if len(srcs) > 1 else 0))
             sent[0] += h
         g.remote_dma_fused(tr, local_sem=T.sem.sent)
 
@@ -185,356 +191,515 @@ def rank_program(g, core, T, topo):
         wr[m] = ("ar" + m, arrive)
         total["ar" + m] = arrive
 
-    X, B, F, GG, HH, CH, ID, ONE, TC, UC = T.X, T.B, T.F, T.GG, T.HH, T.CH, T.ID, T.ONE, T.TC, T.UC
-    BN, B0, WBK, WCK, CHK, HK, OF0 = ks("Bn", 4), ks("Bo", 6), ks("WB", 3), ks("WC", 4), ks("CH", 5), ks("H", 5), ks("OF0", 6)
+    X, B, GG, ID, ONE, TC, UC, COL, P1 = T.X, T.B, T.GG, T.ID, T.ONE, T.TC, T.UC, T.COL, T.P1
+    BN, B0, OF0 = ks("Bn", 4) + ks("Bx", 4), ks("Bo", 4), ks("OF0", 6)
 
-    dma("S", T.LR[:, 0, :], T.lc[:], w=["LR0"])
-    dma("Y", T.LR[:, 1, :], T.rc[:], w=["LR1"])
     dma("S", T.RC[:, 0, :], T.rec[0::2, :], w=["RC0"])
     dma("Y", T.RC[:, 1, :], T.rec[1::2, :], w=["RC1"])
-    dma("Y", T.XR[:], T.x[:], w=["XR"])
+    dma("S", T.LR[:, 0, :], T.lc[:], w=["LR0"])
+    dma("Y", T.LR[:, 1, :], T.rc[:], w=["LR1"])
+    dma("S", T.RTI[:], T.rt[:], w=["RTI"])
+    dma("Y", B[:, NV:2 * NV], T.x[:], w=["XR"])
     dma("Y", X[:, NV + 2560:NV + 3072], T.nw[:], w=["Y0"])
-    dma("Y", T.RTI[:], T.rt[:], w=["RTI"])
-    dma("Y", T.WTI[:, 0:1], T.wt[:], w=["WTI"])
 
+    iota(T.PI[:, 0:6], [[0, 6]], 0, 1, flt=False, w=["PI"])
     ms(T.ZT[:], 0.0, w=["ZT"])
+    ts(T.PK[:, 0:1], T.PI[:, 0:1], 15, Op.bitwise_and, r=["PI"], w=["PK"])
     ms(ONE[:], 1.0, w=["ONE"])
-    iota(T.PI[:, 0:1], [[0, 1]], 0, 1, flt=False, w=["PI"])
-    iota(T.SV[:, 0:5], [[-1, 5]], 4, w=["SV"])
-    iota(T.LAM[0:32], [[1, 6], [0, 6]], 0, w=["LAM"])
-    iota(T.FC[:, 5, :], [[1, 192]], -256, w=["FC5"])
-    iota(UC[0:32, :, :, 0:5], [[0, 180]], 0, w=["UC"])
-    iota(TC[0:32, :, :, 14:16], [[0, 36], [-19200, 2]], 19200, w=["TCr"])
-    for s in range(5):
-        iota(UC[0:32, s + 1:6, s + 1:6, s], [[0, (5 - s) * (5 - s)]], 19200, r=["UC"], w=["UC%d" % s])
-    iota(TC[0:32, 1:6, 1:6, 14], [[0, 25]], int(TB), w=["TCr"])
-    for s in range(4):
-        iota(UC[0:32, s + 2:6, s + 2:6, s], [[0, (4 - s) * (4 - s)]], int(TB) + 512 * (s + 1), w=["UC%d" % s])
+    ts(COL[:, 0:1], T.PK[:, 0:1], 4.0, Op.is_equal, r=["PK"], w=["COL0"])
+    ms(T.SG[:], 1.0, w=["SG"])
+
+    def fill(cs):
+        for i in cs:
+            act(B[:, i * K:(i + 1) * K], T.ZT[:], bias=COL[:, 0:1], r=["ZT", "COL0"], w=["Bz%d" % i])
+
+    fill(range(6))
+    act(B[:, 0:1], T.ZT[:, 0:1], Act.Copy, r=["ZT"], w=["Bz0"])
+    iota(T.SV[0:32], [[0, 12], [-1, 6]], -4, w=["SV"])
+    iota(T.LAM[0:32], [[0, 2], [1, 6], [0, 6]], -9, w=["LAM"])
     sel(ID[:], ONE[:], [[-1, 128]], Op.is_equal, 0, 1, r=["ONE"], w=["ID"])
-    sel(T.W1[:], ONE[:, :, 0:4], [[-16, 8], [0, 4]], Op.is_ge, 0, 1, r=["ONE"], w=["W1"])
-    sel(T.WB[:, 0:4, :], ONE[:, :, 0:4], [[-16, 8], [-1, 4]], Op.is_equal, 0, 1, r=["ONE"], w=["WB0"])
-    sel(T.WA[:], T.W1[:], [[16, 8], [0, 4]], Op.is_ge, 15, -1, r=["W1"], w=["WA"])
-    sel(T.WB[:, 6:10, :], ONE[:, :, 0:4], [[-1, 4], [-16, 8]], Op.is_equal, -2, 1, r=["ONE"], w=["WB2"])
-    sel(T.W2[:], ONE[:, :, 0:2], [[-1, 2], [-16, 8]], Op.is_equal, 0, 1, r=["ONE"], w=["W2"])
-    for i in range(6):
-        act(B[:, i * K:(i + 1) * K], T.ZT[:], Act.Copy, r=["ZT"], w=["Bz%d" % i])
-    ts(T.PJ[:, 5:6], T.PI[:, 0:1], 15, Op.bitwise_and, r=["PI"], w=["PJ5"])
-    for i in range(5):
-        ts(T.PJ[:, i:i + 1], T.PI[:, 0:1], 4 if i == 0 else i - 1, Op.logical_shift_right, 1, Op.bitwise_and, r=["PI"], w=["PJ%d" % i])
-    ms(T.FH[:, 0:1], 9.0, w=["FH0"])
-    ms(T.FL[:, 0:1], 9.0, w=["FL0"])
-    cp(T.COL[:, 0:1], T.PJ[:, 5:6], r=["PJ5"], w=["COL0"])
-    cp(T.AH[:, 0:5], T.PJ[:, 0:5], r=ks("PJ", 5), w=["AH"])
-    ms(T.THR[:, :, 0:8], -8.5, w=["THR0"])
-    ts(T.COL[:, 1:2], T.COL[:, 0:1], 0.5, Op.is_gt, r=["COL0"], w=["COL1"])
-    ts(T.COL[:, 2:3], T.COL[:, 0:1], 192.0, Op.mult, 256.0, Op.add, r=["COL0"], w=["COL2"])
-    ts(T.AL[:, 0:5], T.AH[:, 0:5], -1.0, Op.mult, 1.0, Op.add, r=["AH"], w=["AL"])
-    tt(T.DH[:, 0:5], T.AH[:, 0:5], T.SV[:, 0:5], Op.mult, r=["AH", "SV"], w=["DH"])
-    ms(T.THR[:, :, 8:16], 8.5, w=["THR1"])
-    tt(T.DL[:, 0:5], T.AL[:, 0:5], T.SV[:, 0:5], Op.mult, r=["AL", "SV"], w=["DL"])
-    ts(T.FC[:, 4, :], T.ZT[:, 0:192], T.COL[:, 2:3], Op.add, r=["ZT", "COL2"], w=["FC4"])
-    scan(T.FH[:, 1:6], T.AL[:, 0:5], T.DH[:, 0:5], 9.0, Op.mult, Op.add, r=["AL", "DH"], w=["FH"])
-    scan(T.FL[:, 1:6], T.AH[:, 0:5], T.DL[:, 0:5], 9.0, Op.mult, Op.add, r=["AH", "DL"], w=["FL"])
-    ts(T.FC[:, 4:6, 0:1], T.FC[:, 4:6, 0:1], T.COL[:, 1:2], Op.mult, r=["COL1"], w=["FC4", "FC5"])
-    ts(T.VH[:, 0:6], T.FH[:, 0:6], 512.0, Op.mult, TB, Op.add, r=["FH", "FH0"], w=["VH"])
-    ts(T.VL[:, 0:6], T.FL[:, 0:6], 512.0, Op.mult, TB, Op.add, r=["FL", "FL0"], w=["VL"])
-    ms(T.ZC[:], 0.0, w=["ZC"])
-    tt(T.MH[:, 0:5], T.VH[:, 0:5], T.AH[:, 0:5], Op.mult, r=["VH", "AH"], w=["MH"])
-    tt(T.ML[:, 0:5], T.VL[:, 0:5], T.AL[:, 0:5], Op.mult, r=["VL", "AL"], w=["ML"])
-    for p in range(6):
-        i = 5 - p
-        ts(TC[0:32, :, p, 10], T.LAM[0:32, :, p], T.FL[0:32, i:i + 1], Op.is_gt, T.VL[0:32, i:i + 1], Op.mult,
-           r=["LAM", "FL", "FL0", "VL"], w=["TCm%d" % (2 * p)])
-        ts(TC[0:32, :, p, 11], T.LAM[0:32, :, p], T.FH[0:32, i:i + 1], Op.is_gt, T.VH[0:32, i:i + 1], Op.mult,
-           r=["LAM", "FH", "FH0", "VH"], w=["TCm%d" % (2 * p + 1)])
+    A3, FF = T.A3, T.FF
+    ms(T.PJ[0:32, 0::6], 0, w=["PJ0"])
+    for i in range(1, 6):
+        ts(T.PJ[0:32, i::6], T.PI[0:32, 0:6], 4 if i == 1 else i - 2, Op.logical_shift_right, 1, Op.bitwise_and, r=["PI"], w=["PJ%d" % i])
+    ms(T.SG[:, :, 0:2], -1.0, w=["SG"])
+    sel(T.WC[:], T.SG[:], [[-16, 8], [0, 8]], Op.is_ge, 0, 1, r=["SG"], w=["WC"])
+    sel(T.WC[:], T.WC[:], [[16, 8], [0, 8]], Op.is_ge, 15, -1, w=["WC"])
 
-    ts(T.LR[:, :, 0:1], T.LR[:, :, 0:1], T.COL[:, 1:2], Op.mult, r=["COL1"], w=["LR0", "LR1"])
-    cp(T.FC[:, 0:4:2, :], T.LR[:], r=["LR0", "LR1"], w=["FC0", "FC2"])
-    tt(T.FC[:, 1:4:2, :], T.LR[:], T.FC[:, 0:4:2, :], Op.subtract, r=["LR0", "LR1", "FC0", "FC2"], w=["FC1", "FC3"])
-    for f in (0, 2, 1, 3, 4, 5):
-        dma("Y", B[f::16, 0:NV], T.FC[:, f, :], r=["FC%d" % f] + ks("Bz", 6), w=["Bo%d" % f])
-    for h in range(2):
-        cp(T.RF[:, :, h, :], T.RC[:, h, :], r=["RC%d" % h], w=["RF%d" % h])
-    ts(T.COL[:, 5:6], T.PI[:, 0:1], 63.5, Op.is_gt, 256.0, Op.mult, r=["PI"], w=["COL5"])
-    op("V", lambda: V.transpose(T.RT[:], T.RF[:]), r=["RF0", "RF1"], w=["RT"])
-    ms(T.WQ[:], 0.0, w=["WQ"])
-    ts(T.COL[:, 3:4], T.COL[:, 5:6], 2560.0, Op.add, r=["COL5"], w=["COL3"])
-    for k in range(6):
-        cp(T.OF0[:, k::6], T.RT[:, 32 * k:32 * k + 32], r=["RT"], w=["OF0%d" % k])
+    def picks(W, key, rows):
+        a, b, c, d = rows
+        sel(W[:, :, 0:2], ONE[:, :, 0:2], [[-16, 8], [a - b, 2]], Op.is_equal, -a, 1, r=["ONE"], w=[key + "0"])
+        sel(W[:, :, 2:4], ONE[:, :, 0:2], [[-16, 8], [c - d, 2]], Op.is_equal, -c, 1, r=["ONE"], w=[key + "1"])
+        sel(W[:, :, 4:6], W[:, :, 0:2], [[-16, 8], [c - d, 2]], Op.not_equal, -c, 1, fill=-1.0, r=[key + "0"], w=[key + "2"])
+        sel(W[:, :, 6:8], ONE[:, :, 0:2], [[-16, 8], [-1000, 2]], Op.is_equal, -4, 1, r=["ONE"], w=[key + "3"])
+
+    picks(T.WB, "WB", (0, 1, 2, 3))
+    iota(UC[0:32, :, :, 0:5], [[0, 180]], 0, w=["UC"])
     for s in range(5):
-        i = 4 - s
-        act(TC[0:32, :, s + 1:6, 2 * s], UC[0:32, :, s + 1:6, s], scale=T.AH[0:32, i:i + 1], r=["UC%d" % s, "AH"], w=["TCu%d" % (2 * s)])
-        act(TC[0:32, :, s + 1:6, 2 * s + 1], UC[0:32, :, s + 1:6, s], scale=T.AL[0:32, i:i + 1], r=["UC%d" % s, "AL"], w=["TCu%d" % (2 * s + 1)])
-    act(X[:, 16 * XV:NV], T.XR[:].indirect(T.OF0[:, XV:192]), Act.Copy, r=["XR"] + OF0, w=["XS"])
-    ts(T.WN[:], T.WA[:], -1.0, Op.mult, r=["WA"], w=["WN"])
-    tt(T.WB[:, 4:6, :], T.W2[:], T.WB[:, 6:8, :], Op.subtract, r=["W2", "WB2"], w=["WB1"])
-    cp(T.WC[:, 0:2, :], T.WA[:, :, 0], r=["WA"], w=["WC0"])
-    cp(T.WC[:, 2:4, :], T.WA[:, :, 0], r=["WA"], w=["WC1"])
-    cp(T.WC[:, 4:12, 2:4], T.WA[:, :, 0:2], r=["WA"], w=["WC2"])
-    cp(T.WC[:, 4:12, 0:2], T.WN[:, :, 0:2], r=["WN"], w=["WC3"])
-    cp(X[:, 0:16 * XV], T.XR[:].indirect(T.OF0[:, 0:XV]), r=["XR"] + OF0, w=["XV"])
-    cp(T.OFA[:], T.RTI[:], r=["RTI"], w=["OFA"])
-    ms(X[:, 0:1], 0.0, w=["XV"])
-    dma("Y", B[:, 3072:6144], B[:, 0:3072], r=B0, w=["Bi0"])
-    dma("Y", B[:, 6144:9216], B[:, 0:3072], r=B0, w=["Bi1"])
+        iota(UC[0:32, s + 1:6, 0:5 - s, s], [[0, (5 - s) * (5 - s)]], 19200, r=["UC"], w=["UC%d" % s])
+    for s in range(4):
+        iota(UC[0:32, s + 2:6, 0:4 - s, s], [[0, (4 - s) * (4 - s)]], int(TB) + 512 * (s + 1), w=["UC%d" % s])
+    cp(A3[0:32, 36:72], T.PJ[0:32], r=ks("PJ", 6), w=["AH"])
+    ts(COL[:, 1:2], T.PK[:, 0:1], 0.5, Op.is_gt, r=["PK"], w=["COL1"])
+    for c in (0, 72):
+        ts(A3[0:32, c:c + 36], A3[0:32, 36:72], -1.0, Op.mult, 1.0, Op.add, r=["AH"], w=["AL%d" % c])
+    ts(COL[:, 5:6], T.PI[:, 0:1], 63.5, Op.is_gt, 256.0, Op.mult, r=["PI"], w=["COL5"])
+    ms(A3[0:32, 0::6], 0.0, w=["AH", "AL0", "AL72"])
+    ms(T.ZC[:], 0.0, w=["ZC"])
+    tt(T.DD[0:32], A3[0:32, 36:108], T.SV[0:32], Op.mult, r=["AH", "AL72", "SV"], w=["DD"])
+    ts(COL[:, 2:3], COL[:, 5:6], 2560.0, Op.add, r=["COL5"], w=["COL2"])
+    scan(FF[0:32], A3[0:32, 0:72], T.DD[0:32], 0.0, Op.mult, Op.add, r=["AL0", "DD"], w=["FF"])
+    ts(COL[:, 3:4], COL[:, 5:6], 2560.0 + 9216, Op.add, r=["COL5"], w=["COL3"])
+    tt(T.MK[0:32], T.LAM[0:32], FF[0:32], Op.is_gt, r=["LAM", "FF"], w=["MK"])
+    ts(T.VV[0:32], FF[0:32], 512.0, Op.mult, TB + 9 * 512, Op.add, r=["FF"], w=["VV"])
+    ms(T.WQ[:], 0.0, w=["WQ"])
+    tt(T.MX[0:32, 0:71], T.VV[0:32, 0:71], A3[0:32, 37:108], Op.mult, r=["VV"], w=["MX"])
 
-    def table_hung(ss):
-        for s in ss:
-            i = 4 - s
-            ts(TC[0:32, :, 0:s + 1, 2 * s], T.LAM[0:32, :, 0:s + 1], T.FH[0:32, i:i + 1], Op.is_gt, T.MH[0:32, i:i + 1], Op.mult,
-               r=["LAM", "FH", "FH0", "MH"], w=["TCh%d" % (2 * s)])
-            ts(TC[0:32, :, 0:s + 1, 2 * s + 1], T.LAM[0:32, :, 0:s + 1], T.FL[0:32, i:i + 1], Op.is_gt, T.ML[0:32, i:i + 1], Op.mult,
-               r=["LAM", "FL", "FL0", "ML"], w=["TCh%d" % (2 * s + 1)])
+    def table_hung():
+        for d in range(2):
+            tt(TC[0:32, :, :, 11 - d], T.MK[0:32, 36 * d:36 * d + 36], T.VV[0:32, 36 * d:36 * d + 36], Op.mult, r=["MK", "VV"], w=["TCm%d" % d])
+        for s in range(5):
+            for d in range(2):
+                c = 36 * d + 4 - s
+                ts(TC[0:32, :, 5 - s:6, 2 * s + d], T.LAM[0:32, 0:6, 5 - s:6], FF[0:32, c:c + 1], Op.is_gt, T.MX[0:32, c:c + 1], Op.mult,
+                   r=["LAM", "FF", "MX"], w=["TCh%d" % (2 * s + d)])
 
-    def table_alias():
-        cp(TC[0:32, :, 1:6, 12:14], TC[0:32, :, 1:6, 0:2], r=["TCu0", "TCu1"], w=["TCa0"])
-        cp(TC[0:32, :, 0, 12:14], TC[0:32, :, 0, 10:12], r=["TCm0", "TCm1"], w=["TCa1"])
+    def table_unhung():
+        for s in range(5):
+            for d in range(2):
+                c = 36 * (1 + d) + 5 - s
+                act(TC[0:32, :, 0:5 - s, 2 * s + d], UC[0:32, :, 0:5 - s, s], scale=A3[0:32, c:c + 1], r=["UC%d" % s, "AH", "AL72"], w=["TCu%d" % (2 * s + d)])
+
+    def table_roots():
+        for j in range(2):
+            cp(TC[0:32, :, 0:5, 12 + 2 * j:14 + 2 * j], TC[0:32, :, 0:5, 0:2], r=["TCu0", "TCu1"], w=["TCa%d" % (2 * j)])
+            cp(TC[0:32, :, 5, 12 + 2 * j:14 + 2 * j], TC[0:32, :, 5, 10:12], r=["TCm0", "TCm1"], w=["TCa%d" % (2 * j + 1)])
 
     def table_turn(j):
-        keys = ks("TCh", 10) + ks("TCu", 10) + ks("TCm", 12) + ["TCa0", "TCa1", "TCr"]
-        mms([(T.PO[0:16, 32 * c:32 * c + 32], TC[0:32, 2 * j + c // 6, c % 6, :], ID[0:32, 0:2, :], True, True) for c in range(12)],
-            r=keys + ["ID"], pb=["PO"])
-        act(T.TT[0:16, 384 * j:384 * j + 384], T.PO[0:16, 0:384], Act.Copy, w=["TT%d" % j], pb=["PO"])
+        pn = ("PO", "PL", "PC1")[j]
+        mms([(T[pn][0:16, c], TC[0:32, 2 * j + c // 6, c % 6, :], ID[0:32, 0:2, :], True, True) for c in range(12)],
+            r=ks("TCh", 10) + ks("TCu", 10) + ks("TCm", 2) + ks("TCa", 4) + ["ID"], pb=[pn])
+        act(T.TT[0:16, 384 * j:384 * j + 384], T[pn][0:16, 0:12], Act.Copy, w=["TT%d" % j], pb=[pn])
+        if j == 2:
+            for q in range(1, 8):
+                dma("Y", T.TT[16 * q:16 * q + 16, :], T.TT[0:16, :], r=ks("TT", 3), w=["TR%d" % q])
 
-    iota(CH[:], [[0, 384]], 0, w=CHK)
-    iota(HH[:], [[0, 384]], 0, w=HK)
-    send("LA0", NV + 2560, ["Y0"])
+    for h in range(2):
+        cp(T.RF[:, :, h, :], T.RC[:, h, :], r=["RC%d" % h], w=["RF%d" % h])
+    ts(T.LR[:, :, 0:1], T.LR[:, :, 0:1], COL[:, 1:2], Op.mult, r=["COL1"], w=["LR0", "LR1"])
+    op("V", lambda: V.transpose(T.RT[:], T.RF[:]), r=["RF0", "RF1"], w=["RT"])
+    for k in range(6):
+        cp(T.OF0[:, k::6], T.RT[:, 32 * k:32 * k + 32], r=["RT"], w=["OF0%d" % k])
+    ts(T.FC[:, 0:4:2, :], T.LR[:], 1.0 + 1.0 / 256, Op.mult, r=["LR0", "LR1"], w=["FC0", "FC2"])
+    for f in (1, 3):
+        tt(T.FC[:, f, :], T.LR[:, f // 2, :], T.FC[:, f - 1, :], Op.subtract, r=["LR0", "LR1", "FC0", "FC2"], w=["FC%d" % f])
+    for f in (0, 2, 1, 3):
+        dma("Y", B[f::16, 0:NV], T.FC[:, f, :], r=["FC%d" % f] + ks("Bz", 6), w=["Bo%d" % f])
+
+    cp(T.OFA[:], T.RTI[:], r=["RTI"], w=["OFA"])
+    ts(T.WP[:], T.WC[:, :, 2:7], 8.0, Op.mult, r=["WC"], w=["WP"])
+    cp(X[:, 0:16 * XV], B[:, NV:2 * NV].indirect(T.OF0[:, 0:XV]), r=["XR"] + OF0, w=["XV"])
+    act(X[:, 16 * XV:NV], B[:, NV:2 * NV].indirect(T.OF0[:, XV:192]), Act.Copy, r=["XR"] + OF0, w=["XS"])
+    ms(X[:, 0:1], 0.0, w=["XV"])
+    dma("Y", T.WTI[:, 0:1], T.wt[:], w=["WTI"])
+
+    iota(T.LN[:], [[0, 8], [1, 4]], 0, 4, w=["LN"])
     iota(T.ZR[:], [[0, 288]], 0, w=["ZR0", "ZR1"])
-    iota(T.X4[:], [[0, 8], [1, 4]], 0, 4, w=["X4"])
-    iota(T.RM2[:], [[0, 192]], 2, w=["RM2"])
-    iota(T.RM[:], [[0, 192]], 1, w=["RM"])
-    iota(T.ZI[:], [[0, 432]], 0, w=ks("ZI", 3))
-    iota(T.RM2[:, 0::6], [[0, 32]], 0, w=["RM2"])
-    iota(T.RM[:, 0::6], [[0, 32]], 0, w=["RM"])
-    iota(T.JLO[:], [[0, 2], [1, 256]], 0, w=["JLO"])
-    iota(T.FA[:, :, 16:64], [[0, 384]], 0, w=["FAz"])
-    sel(T.I12[:], ONE[:, :, 0:12], [[-16, 8], [-1, 12]], Op.is_equal, 0, 1, r=["ONE"], w=["I12"])
-    iota(T.SH[:, :, 8:16], [[0, 64]], 0, w=["SH0"])
-    iota(T.SL[:, :, 8:16], [[0, 64]], 0, w=["SL0"])
-    sel(T.SH[:, :, 0:8], ONE[:, :, 0:8], [[-16, 8], [-1, 4], [1000, 2]], Op.is_equal, -12, 1, r=["ONE"], w=["SH1"])
-    sel(T.SL[:, :, 0:8], ONE[:, :, 0:8], [[-16, 8], [-1, 4], [1000, 2]], Op.is_equal, -1012, 1, r=["ONE"], w=["SL1"])
+    iota(T.W4[:], [[0, 32], [-1, 4]], 5, w=["W4"])
+    iota(T.ZI[:], [[0, 576]], 0, w=ks("ZI", 4))
+    iota(T.IDP[:], [[0, 128]], 32, w=["IDP"])
+    sel(T.IDP[:], T.IDP[:], [[-1, 128]], Op.is_equal, 0, 1, w=["IDP"])
+    if 0 not in FOLD:
+        send("LA0", [(X, NV + 2560)], ["Y0"] + B0)
+    iota(T.F[:, 6::8, 0::2], [[0, 64]], 0, w=["Fz0"])
+    iota(T.F[:, 7::8, 0::2], [[0, 64]], 0, w=["Fz1"])
+    iota(T.J0[:], [[0, 4], [1, 128]], 0, w=["J0"])
+    sel(T.IDM[:], ID[:], [[0, 8], [-1, 16]], Op.is_ge, 11, 0, r=["ID"], w=["IDM"])
+    iota(T.F[:, 5::8, :], [[0, 128]], 0, w=["F5"])
+    picks(T.WR, "WR", (12, 14, 13, 15))
 
-    def wrap(Z, parts, pn, c0, keys):
-        lst = [(T[pn][:, c0:c0 + 32], Z[:, p, 3 - e:35 - e, :], ID[:, :, e::4]) for p in parts for e in range(4)]
-        mms([a + (i == 0, i == len(lst) - 1) for i, a in enumerate(lst)], r=keys + ["ID"], pb=[pn])
+    def round1_constants():
+        sel(T.SE0[:], ONE[:, :, 0:12], [[-16, 8], [-1, 12]], Op.is_equal, 0, 1, r=["ONE"], w=["SE0"])
+        for W, key, c in ((T.SA, "SA", 12), (T.SB, "SB", 14)):
+            iota(W[:], [[0, 128]], 0, w=[key])
+            sel(W[:, :, c:c + 2], ONE[:, :, 0:2], [[-16, 8], [-1, 2]], Op.is_equal, -10, 1, r=["ONE"], w=[key])
 
-    PU = T.P3[:, 64:96]
+    def round2_constants():
+        for W, key in ((T.SE1, "SE1"), (T.SE2, "SE2")):
+            sel(W[:, :, 2:12], ONE[:, :, 0:10], [[-16, 8], [-1, 10]], Op.is_equal, 0, 1, r=["ONE"], w=[key])
+        iota(T.SE1[:, :, 0:2], [[0, 16]], 0, w=["SE1m"])
+        sel(T.SE2[:, :, 0:2], ONE[:, :, 0:2], [[-16, 8], [-1, 2]], Op.is_equal, -12, 1, r=["ONE"], w=["SE2m"])
+        sel(T.SE2[:, :, 0:2], T.SE2[:, :, 0:2], [[-16, 8], [-1, 2]], Op.not_equal, -14, 1, fill=1.0, w=["SE2m"])
+        for W, key, at, lo in ((T.I12, "I12", 2, True), (T.SM, "SM", -10, False)):
+            sel(W[:, 0:24, :], ONE[:, 0:3, :], [[-16, 8], [-1, 6]], Op.is_equal, at, 1, r=["ONE"], w=[key])
+            sel(W[:, 0:24, :], W[:, 0:24, :], [[0, 8], [1 if lo else -1, 6]], Op.is_ge, -2 if lo else 1, 0, w=[key])
+            iota(W[:, 24:64 - 32 * lo, :], [[0, 80 - 64 * lo]], 0, w=[key + "z"])
+        sel(T.I12[:, 32:64, :], ONE[:, 0:4, :], [[-16, 8], [-1, 8]], Op.is_equal, -4, 1, r=["ONE"], w=["I12m"])
+        iota(T.F2[:, 24:32, :], [[0, 128]], 0, w=["F2r"])
 
-    def weigh(src, rs, keys, first=False, final=False):
-        mms([(PU, T.WQ[:, 15 - r:143 - r], src[:, :, r], first and r == 0, final and r == 15) for r in rs], r=["WQ"] + keys, pb=["P3"])
+    def wrap(Z, np_, parts, pn, c0, keys, first=True, final=True, I=ID, ik="ID"):
+        lst = [(T[pn][:, c0:c0 + 32], Z[:, 3 - e:35 - e, p::np_], I[:, :, e::4]) for p in parts for e in range(4)]
+        mms([a + (first and i == 0, final and i == len(lst) - 1) for i, a in enumerate(lst)], r=keys + [ik], pb=[pn])
+
+    PU = T.PX[:, 64:96]
+
+    def count(A, ak, pn):
+        mms([(T[pn][:, 0:8, :, 2 * b:2 * b + 2], A[:, b::4], T.WC[:], True, True) for b in range(4)], r=ak + ["WC"], pb=[pn])
+
+    def sides(lo, hi, pn, klo, khi):
+        ts(hi, T[pn][:, 0:8, 1, :], 8.5, Op.is_gt, w=[khi], pb=[pn])
+        ts(lo, T[pn][:, 0:8, 0, :], -8.5, Op.is_gt, w=[klo], pb=[pn])
 
     offs = ["OFA", "OFB"]
     cur = [0]
-    ZW = T.ZC[:, :, 3:35:4, :]
-    PN = ["P1a", "P1b"] * 3
-    CN = ["PH", "PL", "PH", "PL", "PH", "P2"]
+    ZW = T.ZC[:, 3:35:4, :]
+    ZR0, ZR1 = T.ZR[:, 3:35:4, 0::2], T.ZR[:, 3:35:4, 1::2]
+    WBK, WRK, HK, AK = ks("WB", 4), ks("WR", 4), ks("HO", 4), ks("A5", 4)
+
+    def zi(p):
+        return T.ZI[:, 3:35:4, p::4]
+
+    def records(t):
+        return ["XV", "XS"] + ["R%d_%d" % (u, s) for u in range(t) for s in range(6)] + ks("Y", t)
+
+    def look(t, c0, c1):
+        Bt = NV + 3072 * t
+        tt(T.A5[:, 16 * c0:16 * c1], X[:, 0:Bt].indirect(T.OFC[:, c0:c1]), X[:, Bt + 2560 + 16 * c0:Bt + 2560 + 16 * c1], Op.is_gt,
+           r=records(t) + ["OFC", "Y%d" % t], w=AK[c0 // 8:c1 // 8])
+
+    def look_end(pn, where):
+        sides(T.G5[:, :, 0:8], T.G5[:, :, 8:16], pn, "G50", "G51")
+        if where is None:
+            for p in range(2):
+                tt(T.F[:, 6 + p::8, 0::2], T.G5[:, :, p::2], T[pn][:, 8:16, 0:2, p::2], Op.mult, r=["G50", "G51"], w=["Fz%d" % p], pb=[pn])
+        else:
+            tt(where[0], T.G5[:], T[pn][:, 8:16, 0:2, :], Op.mult, r=["G50", "G51"], w=[where[1]], pb=[pn])
+
     for t in range(3):
         Bt = NV + 3072 * t
         last = t == 2
         yk = "Y%d" % t
         y = X[:, Bt + 2560:Bt + 3072]
-        xk = ["XV", "XS"] + ["R%d_%d" % (u, s) for u in range(t) for s in range(6)] + ks("Y", t)
-        la, lb = "LA%d" % min(t, 1), "LB%d" % min(t, 1)
-        ap, ak = (T.AP, "AP") if t else (T[la], la)
+        xk = records(t)
+        la, lb = "LA%d" % t, "LB%d" % t
+        fold = t in FOLD
 
         def pri(s):
-            lst = []
-            for b in range(4):
-                a, c = Bt + K * s + b, Bt + 2560 + b
-                lst += [(T.PR[:, b::4, s], X[:, a:a + K - b:4], T.WA[:, :, 0], True, False), (T.PR[:, b::4, s], X[:, c:c + K - b:4], T.WN[:, :, 0], False, True)]
-            mms(lst, r=["R%d_%d" % (t, s), yk, "WA", "WN"] + (["R%d_5" % t] if s == 4 else []), pb=["PR"])
-            if s == 0 and not last:
+            if s == 0:
+                c = Bt + 2560
                 lst = []
                 for b in range(4):
-                    a, c = Bt + b, Bt + 2560 + b
-                    o = T.P3[:, 128 + b:256:4]
-                    lst += [(o, X[:, a:a + K - b:4], T.WA[:], True, False), (o, X[:, c:c + K - b:4], T.WN[:], False, True)]
-                mms(lst, r=["R%d_0" % t, yk, "WA", "WN"], pb=["P3"])
-
-        def sides(s, thr, keys):
-            tt(GG[:], T[CN[s]][:, 128:256], thr, Op.is_gt, r=keys, w=["GG"], pb=[CN[s]])
+                    o = T.PX[:, 128 + b:160:4]
+                    lst += [(o, X[:, c + b:c + K:4], T.WP[:, :, 0], True, False), (o, X[:, Bt + b:Bt + K:4], T.WM[:], False, True)]
+                mms(lst, r=["R%d_0" % t, yk, "WP", "WM"], pb=["PX"])
+                return
+            if s == 4 and last:
+                a, c0, keys = T.A5, 0, AK
+            else:
+                a, c0, keys = X, Bt + K * s, ["R%d_%d" % (t, s)] + ["R%d_5" % t] * (s == 4)
+            mms([(T.PR[:, b::4, s], a[:, c0 + b:c0 + K:4], T.WM[:], False, s == 4 and b == 3) for b in range(4)], r=keys + ["WM"], pb=["PR"])
 
         def kept(s):
-            tt(F[:, :, 16 * s:16 * s + 16], GG[:], T[PN[s]][:, 0:4, :], Op.mult, r=["GG"], w=["F%d" % s], pb=[PN[s]])
+            node = T.F[:, s::8, :] if not last else T.F2[:, 1 + s:24:3, :] if s < 2 else T.F5[:, s - 2::4, :]
+            tt(node, GG[:, s], P1[:, 0:8, 0:2, :], Op.mult, r=["GL%d" % s, "GH%d" % s], w=["F%d" % s], pb=["P1"])
 
-        for s in range(6):
+        def differ(high, key):
+            tt(T.TD[:], high, P1[:, 0:8, 2, :], Op.mult, r=[key], w=["TD"], pb=["P1"])
+
+        def choose():
+            tt(ZW, T.TD[:], P1[:, 0:8, 1, :], Op.add, r=["TD"], w=["ZC"], pb=["P1"])
+
+        def root_place():
+            if t == 0:
+                tt(T.TMP[:], T.U0[:], T.LV[:, 0, :], Op.mult, r=["U0", "LV0"], w=["TMP"])
+                ts(ZR0, T.TMP[:], -2560.0 / 192, Op.mult, COL[:, 2:3], Op.add, r=["TMP", "COL2"], w=["ZR0"])
+            elif t == 1:
+                ts(ZR0, T.U0[:], -2560.0, Op.mult, COL[:, 2:3], Op.add, r=["U0", "COL2"], w=["ZR0"])
+            else:
+                ts(T.F2[:, 24:32, 0:8:2], T.U0[:], -2560.0, Op.mult, COL[:, 3:4], Op.add, r=["U0", "COL3", "F2r"], w=["F2h"])
+
+        def root_keeps():
+            for d in range(2):
+                for p in range(2):
+                    tt(T.F[:, 6 + p::8, 8 * d + 1:8 * d + 8:2], T.F[:, 0::8, 8 * d + p:8 * d + 8:2], T.U0[:], Op.mult,
+                       r=["F0", "U0"], w=["FA%d" % (2 * d + p)])
+
+        lives = T.PX[:, 224:256] if t == 0 else T.PX[:, 192:224]
+        jobs = {
+            "WM": lambda: ts(T.WM[:], T.WC[:, :, 0], 8.0, Op.mult, r=["WC"], w=["WM"]),
+            "over": lambda: ts(COL[:, 6:7], T.PK[:, 0:1], 11.5, Op.is_gt, r=["PK"], w=["COL6"]),
+            "under": lambda: ts(T.PK[:, 1:2], T.PK[:, 0:1], 13.5, Op.is_lt, 30720.0, Op.mult, r=["PK"], w=["PK1"]),
+            "both": lambda: tt(COL[:, 6:7], COL[:, 6:7], T.PK[:, 1:2], Op.mult, r=["PK1"], w=["COL6"]),
+            "LV0": lambda: ts(T.LV[:, 0, :], P1[:, 0:8, 3, 0::2], 192.0, Op.mult, w=["LV0"], pb=["P1"]),
+            "ZR1": lambda: ts(ZR1, T.LN[:], COL[:, 5:6], Op.subtract, r=["LN", "COL5"], w=["ZR1"]),
+            "LS1": lambda: ts(T.LS[:, :, 1], T.LN[:], COL[:, 5:6], Op.subtract, r=["LN", "COL5"], w=["LS1"]),
+            "U0": lambda: ts(T.U0[:], T.PX[:, 128:160], 0.5, Op.is_lt, w=["U0"], pb=["PX"]),
+            "T0": lambda: ts(T.T0[:], T.U0[:], -5.0, Op.mult, 6.0, Op.add, r=["U0"], w=["T0"]),
+            "hung": table_hung,
+            "roots": table_roots,
+            "root": root_place,
+            "FA": root_keeps,
+            "OFC": lambda: cp(T.OFC[:], T.PW[:, 0:32], w=["OFC"], pb=["PW"]),
+            "base": lambda: ts(COL[:, 8:9], COL[:, 5:6], float(Bt), Op.add, r=["COL5"], w=["COL8"]),
+            "OFR": lambda: cp(T.OFR[:], T.PX[:, 32:64], w=["OFR"], pb=["PX"]),
+            "ID2": lambda: ts(T.ID2[:], ID[:], 2.0, Op.mult, r=["ID"], w=["ID2"]),
+            "ID4": lambda: ts(T.ID4[:], ID[:], 4.0, Op.mult, r=["ID"], w=["ID4"]),
+            "ID8": lambda: ts(T.ID8[:], ID[:], 8.0, Op.mult, r=["ID"], w=["ID8"]),
+            "IDN": lambda: ts(T.IDN[:], T.IDP[:], -1.0, Op.mult, r=["IDP"], w=["IDN"]),
+            "weight": lambda: cp(COL[:, 4:5], T.WTI[:, 0:1], r=["WTI"], w=["COL4"]),
+            "WQ": lambda: ts(T.WQ[:, 15:143:16], T.WP[:, :, 0], COL[:, 4:5], Op.mult, 0.125, Op.mult, r=["WP", "COL4"], w=["WQ"]),
+            "LS0": lambda: ts(T.LS[:, :, 0], T.PX[:, 192:224], 8.0 / 3, Op.mult, COL[:, 8:9], Op.add, r=["COL8"], w=["LS0"], pb=["PX"]),
+            "RM4": lambda: ts(T.RM4[:], T.W4[:], 4.5, Op.is_lt, r=["W4"], w=["RM4"]),
+            "ZI0": lambda: tt(zi(0), GG[:, 3, :, 8:16:2], T.PX[:, 96:128], Op.add, r=["GH3"], w=["ZI0"], pb=["PX"]),
+            "ZI1": lambda: tt(zi(1), T.LV[:, 4, :], lives, Op.add, r=["LV4"], w=["ZI1"], pb=["PX"]),
+            "F2l": lambda: cp(T.F2[:, 24:32, 1:8:2], T.LS[:, :, 1], r=["LS1", "F2r"], w=["F2l"]),
+            "OFD": lambda: ts(T.OFD[:], T.PW[:, 0:32], Bt - 1.0, Op.min, w=["OFD"], pb=["PW"]),
+            "ON": lambda: ts(T.ON[:], y, float(t), Op.add, r=[yk], w=["ON"]),
+            "J0": lambda: ts(T.J0[:], T.J0[:], COL[:, 6:7], Op.add, r=["COL6"], w=["J0"]),
+            "J1": lambda: ts(T.J1[:], T.J0[:], 128.0, Op.add, r=["J0"], w=["J1"]),
+            "I12N": lambda: ts(T.I12N[:], T.I12[:], -1.0, Op.mult, r=["I12", "I12m", "I12z"], w=["I12N"]),
+            "end": lambda: look_end("PC1", (T.F2[:, 0:24:3, :], "F2m") if last else None),
+        }
+        for h in range(2):
+            jobs["owed%d" % h] = lambda h=h: look(t - 1, 16 * h, 16 * h + 16)
+
+        def early(which):
+            mms([(T.PO[0:64, :, :, i // 2::4], T.F2[:, :, i::8], ID[:], False, False) for i in which],
+                r=["F0", "F1", "F2m", "F2r", "F2l", "F2h"], pb=["PO"])
+
+        def rows(pn, m, W, key, src, h, first=False, final=False):
+            mms([(T[pn][0:m, 8 * h:8 * h + 8], W[:], T[src][:, 256 * h:256 * h + 256], first, final)], r=[src] + key, pb=[pn])
+
+        def owed_out(pn):
+            act(T.OUE[0:96, :], T[pn][0:96], Act.Copy, w=["OUE"], pb=[pn])
+            c = Bt - 2 * NV - K * last
+            for d, o in enumerate((T.yl, T.yr)):
+                dma("Y", o[:, c:c + NV], T.OUE[d:96:2, :], r=["OUE"], w=["y%d" % d])
+
+        IK, MK = ["I12", "I12m", "I12z"], ["SM", "SMz"]
+        pe = {}
+        for h in range(2):
+            pe["lo%d" % h] = lambda h=h: rows("PL" if last else "PO", 96, T.SE1 if last else T.SE0, ["SE0", "SE1", "SE1m"], "E1", h, first=h == 0)
+            pe["hi%d" % h] = lambda h=h: rows("PL" if last else "PO", 96, T.SE2 if last else T.SE0, ["SE0", "SE2", "SE2m"], "E2", h, final=h == 1)
+            pe["a%d" % h] = lambda h=h: rows("PL", 128, T.SA, ["SA"], "E2", h, first=h == 0)
+            pe["b%d" % h] = lambda h=h: rows("PL", 128, T.SB, ["SB"], "E1", h)
+            pe["m%d" % h] = lambda h=h: rows("PO", 128, T.SM, MK, "E1", h)
+            pe["n%d" % h] = lambda h=h: rows("PO", 128, T.SM, MK, "E2", h)
+        pe["j"] = lambda: rows("PO", 128, T.I12, IK, "J0", 1, first=True)
+        pe["k"] = lambda: mms([(T.PL[:, 0:8], T.IDP[:], T.J0[:, 256:K], True, False)], r=["J0", "IDP"], pb=["PL"])
+        pe["out"] = lambda: owed_out("PL")
+        for i in range(4):
+            pe["e%d" % i] = lambda i=i: early(range(2 * i, 2 * i + 2))
+
+        def side(s, kind):
+            for name in SIDE[t].get("%d%s" % (s, kind), "").split():
+                pe[name]()
+
+        def gap(s, kind):
+            for name in GAPS[t].get("%d%s" % (s, kind), "").split():
+                jobs[name]()
+
+        for s in range(5):
             on = offs[cur[0]]
             off = T[on]
-            pn, cn = PN[s], CN[s]
-            P1, PC = T[pn], T[cn]
-            if s == 0 and t:
-                xw, xr, bw, bk = T.XA[:], ["XA"], T.BA[:], ["BA"]
-            else:
-                xw, xr, bw, bk = X[:, 0:Bt], xk, B[:, 0:Bt], B0 + (BN if t else [])
             r0 = Bt + K * s
-            if s == 4:
-                cp(X[:, r0:r0 + 256], xw.indirect(off[:, 0:16]), r=xr + [on], w=["R%d_4" % t])
-                act(X[:, r0 + 256:r0 + K], xw.indirect(off[:, 16:32]), Act.Copy, r=xr + [on], w=["R%d_5" % t])
-                if not last:
-                    send(lb, r0, ["R%d_4" % t, "R%d_5" % t])
-            tt(T.A[:], xw.indirect(off[:]), y, Op.is_gt, r=xr + [on, yk], w=["A"])
-            if s < 5:
-                act(T.BT[:], bw.indirect(off[:]), Act.Copy, r=bk + [on], w=["BT"])
+            if s == 0 and t:
+                xw, xr, bw, bk, wb, wk = T.XA[:], ["XA"], T.E1[:], ["E1"], T.WR, WRK
+            else:
+                far = r0 if s == 4 and not last else Bt
+                xw, xr = X[:, 0:far], xk + (ks("R%d_" % t, 4) if far > Bt else [])
+                bw, bk, wb, wk = B[:, 0:Bt], B0 + BN, T.WB, WBK
+            if s == 4 and last:
+                tt(T.A5[:], xw.indirect(off[:]), y, Op.subtract, r=xr + [on, yk], w=AK)
+                ts(T.A[:], T.A5[:], 0.5, Op.is_gt, r=AK, w=["A"])
+            else:
+                if s == 4:
+                    c = 16 * X4V
+                    cp(X[:, r0:r0 + c], xw.indirect(off[:, 0:X4V]), r=xr + [on], w=["R%d_5" % t])
+                    act(X[:, r0 + c:r0 + K], xw.indirect(off[:, X4V:32]), Act.Copy, r=xr + [on], w=["R%d_4" % t])
+                    more = [(T.ON, 0) if t else (X, Bt + 2560)] if fold else []
+                    send(lb, [(X, r0)] + more, ["R%d_4" % t, "R%d_5" % t, yk] + ["ON"] * t)
+                    (round1_constants, round2_constants)[t]()
+                tt(T.A[:], xw.indirect(off[:]), y, Op.is_gt, r=xr + [on, yk], w=["A"])
+            bn = "OFD" if s == 4 and not last else on
+            act(T.BT[:], bw.indirect(T[bn][:]), Act.Copy, r=bk + [bn], w=["BT"])
             if s < 4:
                 act(X[:, r0:r0 + K], xw.indirect(off[:]), Act.Copy, r=xr + [on], w=["R%d_%d" % (t, s)])
-            if s == 4 and not last:
-                act(T.XA[:], X[:, Bt:Bt + 3072].indirect(T.OFR[:]), Act.Copy, r=ks("R%d_" % t, 6) + [yk, "OFR"], w=["XA"])
-            if s == 5:
-                for h in range(2):
-                    act(T.HO[:, 256 * h:256 * h + 256], T.TT[:].indirect(T.OFI[:, 16 * h:16 * h + 16]), Act.Relu,
-                        bias=Bt + 256.0 * h - TB, r=ks("TT", 3) + ks("TR", 8) + ["OFI"], w=["HO%d" % h])
-                for d in range(4):
-                    act(T.TH5[:, :, 4 * d:4 * d + 4], T.EA[:, 4::6], bias=183.5 + 17 * (d // 2), scale=-1.0, r=["EA"], w=["TH5%d" % d])
-                for d in range(4):
-                    act(T.C5[:, :, 4 * d:4 * d + 4], T.ZC[:, d % 2, 3:35:4, :], Act.Copy, r=["ZC"], w=["C5%d" % d])
-                if t == 1:
-                    act(T.AP[:], T[la][:], bias=float(t), r=[la], w=["AP"])
-                if t == 0:
-                    weigh(ap, range(16), [ak], first=True)
-            if t and s < 2:
-                act(T.OUT[0:96, 256 * s:256 * s + 256], T.PO[0:96, 256 * s:256 * s + 256], Act.Copy, w=[("OUT", "OUTb")[s]], pb=["PO"])
-                if s:
-                    dma("Y", T.yl[:, Bt - 2 * NV:Bt - NV], T.OUT[0:96:2, :], r=["OUT", "OUTb"])
-                    dma("Y", T.yr[:, Bt - 2 * NV:Bt - NV], T.OUT[1:96:2, :], r=["OUT", "OUTb"])
-            if 1 <= s <= 4:
+
+            if t == 0 and s == 0:
+                table_unhung()
+
+            def children():
+                mms([(P1[:, 0:8, :, 2 * b:2 * b + 2], T.BT[:, b::4], wb[:], True, True) for b in range(4)], r=["BT"] + wk, pb=["P1"])
+
+            if s:
                 pri(s - 1)
-            if s == 4:
-                pri(4)
-            if t == 0 and s in (1, 2, 3):
-                table_turn(s - 1)
-                if s == 3:
-                    for q in range(1, 8):
-                        dma("Y", T.TT[16 * q:16 * q + 16, :], T.TT[0:16, :], r=ks("TT", 3), w=["TR%d" % q])
-            mms([(PC[:, 64 + b:256:4], T.A[:, b::4], T.WC[:], True, True) for b in range(4)], r=["A"] + WCK, pb=[cn])
-            if s < 5:
-                nq = 10 if s == 0 else 8
-                mms([(P1[:, 0:nq, b::4], T.BT[:, b::4], T.WB[:, 0:nq, :], True, True) for b in range(4)], r=["BT"] + WBK, pb=[pn])
-
-            if t == 0 and s == 0:
-                table_hung(range(2))
-            if s == 1 and not last:
-                ts(T.U0[:], T.P3[:, 128:256], 0.0, Op.is_ge, w=["U0"], pb=["P3"])
-                a, ka = T.U0[:, :, 0:4], "U0"
-                if t == 0:
-                    ts(T.L0[:], CH[:, 0:192:6], 0.0, Op.is_gt, r=["CH0"], w=["L0"])
-                    ts(T.ZR[:, 1, 3:35:4, :], T.X4[:], T.COL[:, 5:6], Op.subtract, r=["X4", "COL5"], w=["ZR1"])
-                    tt(T.L0[:], T.L0[:], a, Op.mult, r=["U0"], w=["L0"])
-                    a, ka = T.L0[:], "L0"
-                ts(T.ZR[:, 0, 3:35:4, :], a, -2560.0, Op.mult, T.COL[:, 3:4], Op.add, r=[ka, "COL3"], w=["ZR0"])
-            if s == 2 and not last:
-                if t == 0:
-                    cp(T.COL[:, 4:5], T.WTI[:, 0:1], r=["WTI"], w=["COL4"])
-                cp(T.OFR[:], T.P3[:, 32:64], w=["OFR"], pb=["P3"])
-                if t == 0:
-                    ts(T.WQ[:, 15:143:16], T.WA[:, :, 0], T.COL[:, 4:5], Op.mult, r=["WA", "COL4"], w=["WQ"])
-            if s == 3 and not last:
-                scan(T.LS[:], T.EE[:], CH[:], 0.0, Op.mult, Op.add, r=["EE0", "EE1"] + CHK, w=["LS"])
-            if s == 4:
-                ts(T.LT[:], T.PR[:, :, 0:6], 0.0, Op.is_lt, 32.0, Op.mult, r=["PR5"], w=["LT"], pb=["PR"])
-                ts(T.LV[:], CH[:, 0:192], 0.0, Op.is_gt, 192.0, Op.mult, r=CHK, w=["LV"])
-                scan(T.HG[:], T.RM[:], T.LT[:], 0.0, Op.mult, Op.max, r=["RM", "LT"], w=["HG"])
-            if s == 5:
-                tt(T.LO[:], T.HO[:], T.JLO[:], Op.min, r=["HO0", "HO1", "JLO"], w=["LO"])
-                sides(5, T.TH5[:], ks("TH5", 4))
-                if not last:
-                    tt(T.FA[:, :, 0:16], T.U0[:], F[:, :, 0:16], Op.mult, r=["F0", "U0"], w=["FA"])
-                tt(F[:, :, 80:96], GG[:], T.C5[:], Op.mult, r=["GG"] + ks("C5", 4), w=["F5"])
-                break
-
-            ts(HH[:, s::6], PC[:, 64:128], 8.5, Op.is_gt, w=["H%d" % s], pb=[cn])
-            if s < 4:
-                sides(s, T.THR[:], ["THR0", "THR1"])
-            if s == 4:
-                tt(T.EA[:], T.LV[:], T.HG[:], Op.subtract, r=["LV", "HG"], w=["EA"])
-            tt(T.TD[:], HH[:, s::6], P1[:, 4:6, :], Op.mult, r=["H%d" % s], w=["TD"], pb=[pn])
-            if s == 4:
-                ts(T.ZI[:, 2, 3:35:4, :], PC[:, 64:96], 8.5, Op.is_gt, 16.0, Op.mult, w=["ZI2"], pb=[cn])
-            if s == 3 and not last:
-                tt(CH[:, 4::6], T.TD[:], P1[:, 6:8, :], Op.add, r=["TD"], w=["CH4"], pb=[pn])
-                for p in range(2):
-                    ts(T.E4[:, p, :], CH[:, 4:192:6], 0.0, Op.is_equal, r=["CH4"], w=["E4%d" % p])
-                tt(T.Q4[:], T.E4[:], T.LS[:, 3::6], Op.mult, r=["E40", "E41", "LS"], w=["Q4"])
-                tt(ZW, T.Q4[:], CH[:, 4::6], Op.add, r=["Q4", "CH4"], w=["ZC"])
             else:
-                tt(ZW, T.TD[:], P1[:, 6:8, :], Op.add, r=["TD"], w=["ZC"], pb=[pn])
-            wrap(T.ZC, (0, 1), "P2", 0, ["ZC"])
-            if s == 0:
-                cp(CH[:, 0::6], P1[:, 8:10, :], w=["CH0"], pb=[pn])
+                c, nc = Bt + 2560, 5 - last
+                mms([(T.PR[:, b::4, 1:nc], X[:, c + b:c + K:4], T.WP[:, :, 1:nc], b == 0, False) for b in range(4)], r=[yk, "WP"], pb=["PR"])
             if s < 4:
-                kept(s)
-            if s < 3 or (last and s == 3):
-                cp(CH[:, s + 1::6], ZW, r=["ZC"], w=["CH%d" % (s + 1)])
-            if t == 0 and s == 0:
-                table_hung(range(2, 5))
-                table_alias()
-                ms(T.PR[:, :, 5], 0.0, w=["PR5"], pb=["PR"])
-            if s == 2 and not last:
-                for p in range(2):
-                    ts(T.EE[:, 192 * p:192 * p + 192], CH[:, 0:192], 0.0, Op.is_equal, r=CHK, w=["EE%d" % p])
-                ms(T.EE[:, 0::6], 0.0, w=["EE0", "EE1"])
+                side(s, "w")
+            if t == 0 and s in (1, 2):
+                for j in range(2 * s - 2, s + 1):
+                    table_turn(j)
+            if t and s == LOOK[t]:
+                count(T.A5, AK, "PC1")
             if s == 3:
-                scan(T.HS[:], T.RM2[:], HH[:, 0:192], 0.0, Op.mult, Op.add, r=["RM2"] + HK, w=["HS"])
+                lst = [(T.PX[:, 96:128], T["ID%d" % (8 >> u)][:], GG[:, u, :, 8:16:2], u == 0, u == 2) for u in range(3)]
+                lst += [(T.PX[:, 192:224], ID[:], T.LV[:, u, :], u == 1, u == 3) for u in range(1, 4)]
+                if t == 0:
+                    lst += [(lives, ID[:], T.LV[:, u, :], u == 0, u == 3) for u in range(4)]
+                mms(lst, r=ks("GH", 3) + ks("LV", 4) + ["ID2", "ID4", "ID8"], pb=["PX"])
             if s == 4:
-                scan(T.ES[:], T.RM[:], T.EA[:], 0.0, Op.mult, Op.add, r=["RM", "EA"], w=["ES"])
-                cp(T.ZI[:, 0, 3:35:4, :], T.HS[:, 3::6], r=["HS"], w=["ZI0"])
-                ts(T.ZI[:, 1, 3:35:4, :], T.ES[:, 4::6], 160.0, Op.add, r=["ES"], w=["ZI1"])
-                tt(T.X4[:], T.LV[:, 4::6], T.HG[:, 4::6], Op.add, r=["LV", "HG"], w=["X4"])
-                wrap(T.ZI, (2, 0, 1), "P3", 0, ks("ZI", 3))
-                for d in range(4):
-                    act(T.TH4[:, :, 4 * d:4 * d + 4], T.X4[:], bias=183.5 + 17 * (d // 2), scale=-1.0, r=["X4"], w=["TH4%d" % d])
+                break
+            count(T.A, ["A"], "PC0")
+            children()
+            gap(s, "c")
+            if t == 1 and s == 0:
+                if not fold:
+                    send(la, [(T.ON, 0)], ["ON"])
+                for i in (2, 3, 4, 5, 0, 1):
+                    iota(B[:, Bt + K * i:Bt + K * (i + 1)], [[0, K]], 0, r=BN if i < 2 else [], w=["Bf%d" % i])
+            side(s, "m")
+            sides(GG[:, s, :, 0:8], GG[:, s, :, 8:16], "PC0", "GL%d" % s, "GH%d" % s)
+            differ(GG[:, s, :, 8:16], "GH%d" % s)
+            choose()
+            idle = s == 3 and not last
+            wrap(T.ZC, 2, (0, 1), "PW", 0, ["ZC"], final=not idle)
+            if idle:
+                kept(s)
+                for p in range(2):
+                    ts(T.E4[:, :, p], T.ZC[:, 3:35:4, 0::2], 0.5, Op.is_lt, r=["ZC"], w=["E4%d" % p])
+                ts(T.LV[:, 4, :], T.ZC[:, 3:35:4, 0::2], 0.5, Op.is_gt, 192.0, Op.mult, r=["ZC"], w=["LV4"])
+                tt(T.ZR[:, 3:35:4, :], T.E4[:], T.LS[:], Op.mult, r=["E40", "E41", "LS0", "LS1"], w=["ZR0", "ZR1"])
+                wrap(T.ZR, 2, (0, 1), "PW", 0, ["ZR0", "ZR1"], first=False)
+            else:
+                kept(s)
+                ts(T.LV[:, s + 1, :], T.ZC[:, 3:35:4, 0::2], 0.5, Op.is_gt, 192.0, Op.mult, r=["ZC"], w=["LV%d" % (s + 1)])
+            gap(s, "w")
             cur[0] ^= 1
-            cp(T[offs[cur[0]]][:], T.P2[:, 0:32], w=[offs[cur[0]]], pb=["P2"])
+            cp(T[offs[cur[0]]][:], T.PW[:, 0:32], w=[offs[cur[0]]], pb=["PW"])
+            gap(s, "e")
             if s == 1 and not last:
-                wrap(T.ZR, (0, 1), "P3", 32, ["ZR0", "ZR1"])
-            if s == 4:
-                sides(4, T.TH4[:], ks("TH4", 4))
-                cp(T.OFI[:], T.P3[:, 0:32], w=["OFI"], pb=["P3"])
-                kept(4)
+                wrap(T.ZR, 2, (0, 1), "PX", 32, ["ZR0", "ZR1"])
 
-        fk = ks("F", 6) + ["ID"]
+        wrap(T.ZI, 4, (0, 1), "PX", 0, ["ZI0", "ZI1"], final=False)
+        side(4, "w")
+        pri(4)
         if last:
-            hv = ((T.PO, 0), (T.PL, 1))
-            mms([(p[0:96, 0:256], T.I12[:], T.HO[:, 256 * h:256 * h + 256], True, False) for p, h in hv] +
-                [(T.PH[0:8, :], ID[:, :, 14], T.HO[:], True, False)], r=["HO0", "HO1", "I12", "ID"], pb=["PO", "PL", "PH"])
-            mms([(p[0:96, 0:256], T.I12[:], T.LO[:, 256 * h:256 * h + 256], False, False) for p, h in hv], r=["LO"], pb=["PO", "PL"])
-            for h, nm in enumerate(("PO", "PL")):
-                mms([(T[nm][0:96, i // 2:256:4], F[:, :, 4 * (i % 2) + i // 2::8], ID[:, 4 * h:4 * h + 4, :], False, i == 7) for i in range(8)],
-                    r=fk, pb=[nm])
-            mms([(T.PH[0:8, :], ID[:, :, 14], T.LO[:], False, True)], r=["LO"], pb=["PH"])
-            act(T.OUT[0:96, 0:256], T.PO[0:96, 0:256], Act.Copy, w=["OUT"], pb=["PO"])
-            cp(T.OUT[0:96, 256:K], T.PL[0:96, 0:256], w=["OUTb"], pb=["PL"])
-            dma("S", T.yl[:, Bt - NV:Bt], T.OUT[0:96:2, :], r=["OUT", "OUTb"])
-            dma("Y", T.yr[:, Bt - NV:Bt], T.OUT[1:96:2, :], r=["OUT", "OUTb"])
-            cp(T.OUTR[0:8, :], T.PH[0:8, :], w=["OUTR"], pb=["PH"])
-            dma("S", T.yt[:], T.OUTR[0:8, :], r=["OUTR"])
-            break
-        mms([(T.PH[0:96, :], T.I12[:], T.HO[:], True, False), (T.PO[:], T.SH[:], T.HO[:], True, False)], r=["HO0", "HO1", "I12", "SH0", "SH1"], pb=["PH", "PO"])
-        mms([(T.PO[:], T.SL[:], T.LO[:], False, False), (T.PL[0:96, :], T.I12[:], T.LO[:], True, False)], r=["LO", "I12", "SL0", "SL1"], pb=["PL", "PO"])
-        mms([(T.PO[:, b::4], T.FA[:, :, b::4], ID[:], False, b == 3) for b in range(4)], r=["FA", "FAz", "ID"], pb=["PO"])
-        act(T.BA[:], T.PO[:], Act.Copy, w=["BA"], pb=["PO"])
-        for nm, part in (("PH", 0), ("PL", 4)):
-            mms([(T[nm][0:96, b::4], F[:, :, part + b::8], ID[:], False, b == 3) for b in range(4)], r=fk, pb=[nm])
-        if t:
-            weigh(ap, range(16), [ak], first=True)
-        act(T.HI[0:96, :], T.PH[0:96, :], Act.Copy, w=["HI"], pb=["PH"])
-        act(T.LW[0:96, :], T.PL[0:96, :], Act.Copy, w=["LW"], pb=["PL"])
-        for part, nm in enumerate(("HI", "LW")):
-            for side in range(2):
-                dma("Y", B[2 * side + part::16, Bt:Bt + 3072], T[nm][side:96:2, :], r=[nm, "Bi%d" % t], w=["Bn%d" % (2 * side + part)])
+            children()
+        count(T.A, ["A"], "PC0")
+        if not last:
+            children()
+        tt(T.LT[:], T.PR[:, :, 1:5], T.W4[:], Op.min, r=["W4"], w=["LT"], pb=["PR"])
+        scan(T.NH[:], T.RM4[:], T.LT[:], 0.0, Op.mult, Op.max, r=["RM4", "LT"], w=["NH"])
+        if last:
+            sides(T.N4[:], T.H4[:], "PC0", "N4", "H4")
+        ts(zi(2), T.PC0[:, 0:8, 1, 0::2], 8.5, Op.is_gt, 16.0, Op.mult, w=["ZI2"], pb=["PC0"])
+        if last:
+            differ(T.H4[:], "H4")
+        wrap(T.ZI, 4, (2,), "PX", 0, ["ZI2"], first=False, final=False)
+        tt(zi(3), T.NH[:, 3::4], T.T0[:], Op.max, r=["NH", "T0"], w=["ZI3"])
+        wrap(T.ZI, 4, (3,), "PX", 0, ["ZI3"], first=False, I=T.IDP, ik="IDP")
+        if last:
+            choose()
+            wrap(T.ZC, 2, (0, 1), "PW", 0, ["ZC"])
+        else:
+            sides(T.N4[:], T.H4[:], "PC0", "N4", "H4")
+        if t == 1:
+            owed_out("PO")
+        for p in range(2):
+            tt(T.Q4[:, :, p], zi(3), T.LV[:, 4, :], Op.min, r=["ZI3", "LV4"], w=["Q4%d" % p])
+        tt(GG[:, 4, :, 0:8], T.Q4[:], T.H4[:], Op.is_gt, r=["Q40", "Q41", "H4"], w=["GL4"])
+        tt(GG[:, 4, :, 8:16], T.Q4[:], T.N4[:], Op.is_gt, r=["Q40", "Q41", "N4"], w=["GH4"])
+        ts(T.Q5[:], T.Q4[:], 1.0, Op.is_equal, r=["Q40", "Q41"], w=["Q5"])
+        if not last:
+            kept(4)
+        ts(T.OFI[:], T.PX[:, 0:32], 160.0 if t else -32.0, Op.add, w=["OFI"], pb=["PX"])
+        if not last:
+            differ(T.H4[:], "H4")
+        for q in (2, 3, 0, 1):
+            a = (T.HO[:, 128 * q:128 * q + 128], T.TT[:].indirect(T.OFI[:, 8 * q:8 * q + 8]))
+            bias, kw = Bt + 128.0 * (q - (t == 1)) - TB, dict(r=ks("TT", 3) + ks("TR", 8) + ["OFI"], w=["HO%d" % q])
+            if last or q >= 2:
+                act(*a, Act.Relu, bias=bias, **kw)
+            else:
+                ts(*a, bias, Op.add, 0.0, Op.max, **kw)
+        if not last:
+            choose()
+        tt(T.CM[:], ZW, T.Q5[:], Op.mult, r=["ZC", "Q5"], w=["CM"])
+        fk = ks("F", 6) + ["ID"]
 
-        weigh(T[lb], range(16), [lb])
-        for h in range(2):
-            c = slice(8 * h, 8 * h + 8)
-            tt(T.SS[:, :, c], ap[:, :, c], T[lb][:, :, c], Op.add, r=[ak, lb], w=["SS%d" % h])
-            ts(T.MM[:, :, c], T.SS[:, :, c], 15.5, Op.is_gt, -16.0, Op.mult, r=["SS%d" % h], w=["MM%d" % h])
-            weigh(T.MM, range(8 * h, 8 * h + 8), ["MM%d" % h], final=True)
+        def last_child(pn):
+            mms([(T[pn][:, 8:16, d, :], ID[:], T.CM[:], True, True) for d in range(2)], r=["CM", "ID"], pb=[pn])
+
+        if last:
+            lo, hi = slice(0, 256), slice(256, K)
+            jobs["OFC"]()
+            look(t, 0, 32)
+            kept(4)
+            last_child("PC1")
+            mms([(T.PL[:, 0:8], T.IDN[:], T.HO[:, hi], False, True), (T.PO[:, 8:16], T.I12[:], T.HO[:, hi], False, False)],
+                r=HK[2:4] + ["IDN"], pb=["PL", "PO"])
+            act(T.LO[:, hi], T.PL[:, 0:8], Act.Relu, scale=1.0 / 32, w=["LO1"], pb=["PL"])
+            mms([(T.PO[:, 0:8], T.I12[:], T.HO[:, lo], False, False)], r=HK, pb=["PO"])
+            tt(T.LO[:, lo], T.HO[:, lo], T.J0[:, lo], Op.min, r=HK[0:2] + ["J0"], w=["LO0"])
+            count(T.A5, AK, "PC1")
+            mms([(T.PO[:, 8:16], T.I12N[:], T.LO[:, hi], False, False)], r=["LO1", "I12N"], pb=["PO"])
+            mms([(T.PO[:, 0:8], T.I12[:], T.LO[:, lo], False, True)], r=["LO0"], pb=["PO"])
+            act(T.OUT[:], T.PO[:], Act.Copy, w=["OUT"], pb=["PO"])
+            dma("S", T.yl[:, Bt - NV - K:Bt - NV + 2 * K], T.OUT[0:48:2, :], r=["OUT"], w=["y0"])
+            dma("Y", T.yr[:, Bt - NV - K:Bt - NV + 2 * K], T.OUT[1:48:2, :], r=["OUT"], w=["y1"])
+            dma("Y", T.yt[:], T.OUT[48:64:2, :], r=["OUT"])
+            look_end("PC1", (T.F5[:, 3::4, :], "F5"))
+            mms([(T.PR[64:128, 0:16, i // 2::4], T.F5[:, :, i::8], ID[:, 0:4, :], i % 2 == 0, i % 2 == 1) for i in range(8)], r=fk, pb=["PR"])
+            mms([(T.PX[64:128, i // 2:256:4], T.F5[:, :, i::8], ID[:, 4:8, :], i % 2 == 0, i % 2 == 1) for i in range(8)], r=fk, pb=["PX"])
+            tt(T.OUM[64:128, lo], T.PR[64:128, 0:16, :], T.OUT[64:128, lo], Op.add, r=["OUT"], w=["OUM0"], pb=["PR"])
+            tt(T.OUM[64:128, hi], T.PX[64:128, 0:256], T.OUT[64:128, hi], Op.add, r=["OUT"], w=["OUM1"], pb=["PX"])
+            dma("S", T.yl[:, Bt - 4 * K:Bt], T.OUM[64::2, :], r=["OUM0", "OUM1"])
+            dma("Y", T.yr[:, Bt - 4 * K:Bt], T.OUM[65::2, :], r=["OUM0", "OUM1"])
+            break
+
+        def parts(nm, part, first):
+            mms([(T[nm][:, :, :, b::4], T.F[:, :, 2 * b + part::8], ID[:], first and b == 0, not first and b == 3) for b in range(4)],
+                r=fk + ks("FA", 4) + ["Fz0", "Fz1"], pb=[nm])
+
+        act(T.XA[:], X[:, Bt:Bt + 3072].indirect(T.OFR[:]), Act.Copy, r=ks("R%d_" % t, 6) + [yk, "OFR"], w=["XA"])
+        parts("PO", 1, True)
+        for q in (0, 2, 1, 3):
+            mms([(T.PO[:, 4 * q:4 * q + 4], ID[:], T.HO[:, 128 * q:128 * q + 128], False, q == 3)], r=["HO%d" % q], pb=["PO"])
+        mms([(T.PL[:], T.IDM[:], T.HO[:], t == 0, False)], r=HK + ["IDM"], pb=["PL"])
+        parts("PL", 0, False)
+        jn = "J%d" % t
+        gap(4, "a")
+        tt(T.E1[:], T.PO[:], T[jn][:], Op.min, r=[jn], w=["E1"], pb=["PO"])
+        act(T.E2[:], T.PL[:], Act.Copy, w=["E2"], pb=["PL"])
+        for part, nm in ((1, "E1"), (0, "E2")):
+            for side in range(2):
+                dma("Y", B[2 * side + part::16, Bt:Bt + 4096], T[nm][side::2, :], r=[nm, "XV", "XS"] + ks("Bf", 6), w=["Bn%d" % (2 * side + part)])
+        if t:
+            for k, f in enumerate((0, 2, 1, 3)):
+                dma("Y", B[f::16, Bt - K:Bt], T.E2[12 + k::16, :], r=["E2"], w=["Bx%d" % k])
+
         n0 = Bt + 3072 + 2560
-        tt(X[:, n0:n0 + K], T.SS[:], T.MM[:], Op.add, r=ks("SS", 2) + ks("MM", 2), w=["Y%d" % (t + 1)])
-        if t == 0:
-            send("LA1", n0, ["Y1"])
-        mms([(T.PO[0:96, :], ID[0:96, 0:6, :], T.HI[0:96, :], True, False), (T.PO[0:96, :], ID[0:96, 0:6, :], T.LW[0:96, :], False, True)],
-            r=["ID", "HI", "LW"], pb=["PO"])
-        cp(T.UI[:], PU, w=["UI"], pb=["P3"])
+        ss, nk = (T[lb] if fold else T.SS), "Y%d" % (t + 1)
+
+        def weigh(src, rs, keys, first=False, final=False):
+            mms([(PU, T.WQ[:, 15 - r:143 - r], src[:, :, r], first and r == 0, final and r == 15) for r in rs], r=["WQ"] + keys, pb=["PX"])
+
+        if not fold:
+            weigh(T[la], range(16), [la], first=True)
+        wrap(T.ZC, 2, (0, 1), "PW", 0, ["ZC"])
+        last_child("PC1")
+        weigh(T[lb], range(16), [lb], first=fold)
+        for h in range(2):
+            if not fold:
+                tt(T.SS[:, :, h::2], T[la][:, :, h::2], T[lb][:, :, h::2], Op.add, r=[la, lb], w=["SS%d" % h])
+        for h in range(2):
+            ts(T.MM[:, :, h::2], ss[:, :, h::2], 15.5, Op.is_gt, -16.0, Op.mult, r=["SS%d" % h, lb], w=["MM%d" % h])
+            weigh(T.MM, range(h, 16, 2), ["MM%d" % h], final=True)
+        tt(X[:, n0:n0 + K], ss[:], T.MM[:], Op.add, r=["SS0", "SS1", "MM0", "MM1"], w=[nk])
+        cp(T.UI[:], PU, w=["UI"], pb=["PX"])
         ts(T.UJ[:], T.UI[:], K - 1, Op.bitwise_and, r=["UI"], w=["UJ"])
         cur[0] ^= 1
         cp(T[offs[cur[0]]][:], T.UJ[:], r=["UJ"], w=[offs[cur[0]]])

from concourse.bass import DstId, RemoteDMATransfer
from concourse.mybir import AluOpType as Op, ActivationFunctionType as Act

BF, F32, I32, U16 = "bfloat16", "float32", "int32", "uint16"
NV, K = 3072, 512
TB = 16640.0
XV = 86
X4V = 18
FOLD = (1,)
LOOK = (0, 2, 2)
GAPS = ({"0c": "hung", "0w": "WM LV0 ZR1 roots", "1c": "U0 over under root LS1 T0", "1w": "FA base both RM4", "2c": "OFR ID8 ID4 ID2 IDN", "2w": "weight J0", "3c": "LS0 WQ", "3w": "ZI0 ZI1", "3e": "OFD"}, {"0c": "OFC ON ZR1", "0w": "owed0", "1c": "U0 base root T0", "1w": "owed1", "2c": "OFR end", "2w": "FA", "3c": "LS0 J1", "3w": "ZI0 ZI1", "3e": "OFD"}, {"0c": "OFC F2l I12N", "0w": "owed0", "1c": "U0 root T0", "1w": "owed1", "2c": "end", "3w": "ZI0 ZI1"})
SIDE = ({}, {"0m": "lo0", "1w": "lo1", "1m": "hi0", "2w": "hi1 a0", "2m": "a1", "3w": "b0", "3m": "b1"}, {"0w": "lo0 lo1", "0m": "hi0", "1w": "hi1 out", "1m": "j", "2w": "m0 m1", "2m": "n0", "3w": "n1 k", "3m": "e0", "4w": "e1 e2 e3"})
SB = {
    BF: {"X": [9216 + 3072], "B": [9216 + 1024], "TT": [1152], "TC": [6, 6, 16], "UC": [6, 6, 8], "FC": [4, 192],
         "WP": [8, 5], "WM": [8], "WQ": [144], "I12": [64, 2], "I12N": [64, 2], "SM": [64, 2],
         "ZC": [36, 8], "ZR": [36, 8], "ZI": [36, 16], "GG": [5, 8, 16], "G5": [8, 16], "F": [64, 16], "F2": [32, 16],
         "F5": [32, 16], "U0": [32], "T0": [32], "TMP": [32], "LV": [5, 32]},
    F32: {"OUT": [K], "OUM": [K], "OUE": [K], "LAM": [12, 6], "A3": [108], "COL": [16], "RF": [6, 2, 16], "RT": [192], "TD": [32, 2], "LN": [8, 4]},
    I32: {"RC": [2, 96], "LR": [2, 192], "RTI": [32], "WTI": [4], "UI": [32], "UJ": [32], "PI": [8], "PK": [8], "PJ": [36]},
    U16: {"OF0": [192], "OFA": [32], "OFB": [32], "OFC": [32], "OFD": [32], "OFI": [32], "OFR": [32]},
}
SB[BF].update({k: [K] for k in ("XA", "A", "A5", "BT", "ZT", "J0", "J1", "ON", "HO", "LO", "E1", "E2")})
SB[BF].update({k: [32, 16] for k in ("LA0", "LA1", "LB0", "LB1", "SS", "MM")})
SB[BF].update({k: [8, 16] for k in ("ONE", "ID", "IDM", "IDP", "IDN", "ID2", "ID4", "ID8", "SA", "SB")})
SB[BF].update({k: [8, 12] for k in ("SE0", "SE1", "SE2")})
SB[BF].update({k: [8, 8] for k in ("SG", "WC", "WB", "WR")})
SB[BF].update({k: [32, 2] for k in ("H4", "N4", "Q4", "Q5", "CM", "CH", "E4", "LS")})
SB[BF].update({k: [128] for k in ("LT", "W4", "RM4", "NH")})
SB[F32].update({k: [72] for k in ("SV", "DD", "FF", "MK", "VV", "MX")})
SCRATCH = {k: ("sbuf", [128] + sh, d) for d, bufs in SB.items() for k, sh in bufs.items()}
SCRATCH.update({k: ("psum", [128, 16, 4, 8], F32) for k in ("P1", "PC0", "PC1", "PO", "PL")})
SCRATCH.update({k: ("psum", [128, K], F32) for k in ("PW", "PX")})
SCRATCH["PR"] = ("psum", [128, 32, 16], F32)
NDMA = 58
MSGS = [m + str(t) for t in range(2) for m in ("LA", "LB") if m == "LB" or t not in FOLD]
SEMAPHORES = ["cV", "cS", "cP", "cG", "sent"] + ["ar" + m for m in MSGS] + ["d%d" % i for i in range(NDMA)]


def relays_for(src, dst, T, topo):
    if topo.may_write(src, dst):
        return []
    out = {}
    for c in topo.cores_of(src):
        if c != src and T.rank_of(c) is None and topo.may_write(c, dst):
            out.setdefault(topo.die(c), c)
    return sorted(out.values(), key=lambda c: topo.die(c) != topo.die(src))


def bits(engines):
    m = 0
    for e in engines:
        m |= 1 << e
    return m


def relay_program(g, core, T, topo):
    n = len(T.cores)
    for r in range(n):
        src, dst = T.cores[r], T.cores[(r + 1) % n]
        rl = relays_for(src, dst, T, topo)
        if core not in rl:
            continue
        i, w = rl.index(core), 32 // len(rl)
        got = len(topo.engines(src, core)) // len(rl)
        rid, pid = topo.addr(dst, core)
        for m in MSGS:
            g.wait_ge(T.sem["ar" + m], got)
            piece = T[m][:, i * w:(i + 1) * w, :]
            g.remote_dma(piece, piece, T.sem["ar" + m], T.sem.sent, pid, rid, topo.mask(core, dst))
        g.wait_ge(T.sem.sent, len(MSGS) * len(topo.engines(core, dst)))


def rank_program(g, core, T, topo):
    rank = T.rank_of(core)
    if rank is None:
        relay_program(g, core, T, topo)
        return
    n = len(T.cores)
    nxt, prv = T.cores[(rank + 1) % n], T.cores[(rank - 1) % n]
    Q = {"V": g.vector, "S": g.scalar, "P": g.tensor, "G": g, "Y": g.sync}
    cnt = {"V": 0, "S": 0, "P": 0, "G": 0}
    known = {q: {} for q in Q}
    wr, rd, bank, total = {}, {}, {}, {}
    nd = [0]

    def wait(q, toks):
        need = {}
        for s, c in toks:
            if q == "P" and s == "cP":
                continue
            if c > known[q].get(s, 0) and c > need.get(s, 0):
                need[s] = c
        for s, c in need.items():
            Q[q].wait_ge(T.sem[s], c)
            known[q][s] = c

    def deps(q, r, w, pb):
        toks = [wr[k] for k in list(r) + list(w) if k in wr]
        for k in w:
            toks += rd.get(k, [])
        for b in pb:
            toks += [t for e, t in bank.get(b, {}).items() if e != q]
        wait(q, toks)

    def note(q, tok, r, w, pb):
        for k in r:
            rd.setdefault(k, []).append(tok)
        for k in w:
            wr[k] = tok
            rd[k] = []
        for b in pb:
            bank.setdefault(b, {})[q] = tok
        total[tok[0]] = tok[1]

    def op(q, fn, r=(), w=(), pb=()):
        deps(q, r, w, pb)
        cnt[q] += 1
        fn().then_inc(T.sem["c" + q], 1)
        note(q, ("c" + q, cnt[q]), r, w, pb)

    def dma(q, out, in_, r=(), w=(), add=False):
        deps(q, r, w, ())
        s = "d%d" % nd[0]
        nd[0] += 1
        if add:
            Q[q].dma_start(out, in_, accum_op=Op.add, max_dma_last_dim=2048).then_inc(T.sem[s], 16)
        else:
            Q[q].dma_start(out, in_).then_inc(T.sem[s], 16)
        note(q, (s, 16), r, w, ())

    V, S, P = g.vector, g.scalar, g.tensor

    def ts(out, a, s1, o0, s2=None, o1=None, **kw):
        if o1 is None:
            op("V", lambda: V.tensor_scalar(out, a, s1, None, o0), **kw)
        else:
            op("V", lambda: V.tensor_scalar(out, a, s1, s2, o0, o1), **kw)

    def tt(out, a, b, o, **kw):
        op("V", lambda: V.tensor_tensor(out, a, b, o), **kw)

    def cp(out, a, **kw):
        op("V", lambda: V.tensor_copy(out, a), **kw)

    def ms(out, c, **kw):
        op("V", lambda: V.memset(out, c), **kw)

    def scan(out, d0, d1, init, o0, o1, **kw):
        op("V", lambda: V.tensor_tensor_scan(out, d0, d1, init, o0, o1), **kw)

    def act(out, a, f=Act.Identity, bias=0.0, scale=1.0, **kw):
        op("S", lambda: S.activation(out, a, f, bias=bias, scale=scale), **kw)

    def mms(lst, **kw):
        deps("P", kw.get("r", ()), kw.get("w", ()), kw.get("pb", ()))
        for a in lst[:-1]:
            P.matmul(*a)
        op("P", lambda: P.matmul(*lst[-1]), **kw)

    def iota(out, pat, base, cm=0, flt=True, **kw):
        if flt:
            op("G", lambda: g.iota(out, pat, base, cm, allow_small_or_imprecise_dtypes=True), **kw)
        else:
            op("G", lambda: g.iota(out, pat, base, cm), **kw)

    def sel(out, a, pat, o, base, cm, fill=0.0, **kw):
        op("G", lambda: g.affine_select(out, a, pat, o, fill, base, cm), **kw)

    def ks(name, m):
        return [name + str(i) for i in range(m)]

    sent = [0]

    def send(m, srcs, keys):
        deps("G", keys, (), ())
        rl = relays_for(core, nxt, T, topo) or [nxt]
        w, tr = 32 // len(rl), []
        for i, c in enumerate(rl):
            e = topo.engines(core, c)
            h = len(e) // len(rl)
            rid, pid = topo.addr(c, core)
            pieces = [a[:, c0 + 16 * i * w:c0 + 16 * (i + 1) * w] for a, c0 in srcs]
            tr.append(RemoteDMATransfer(dst_ids=[DstId(rid=rid, pnc=pid)], dma_engine_mask=bits(e[i * h:(i + 1) * h]), remote_sem=T.sem["ar" + m],
                                        srcs=pieces, dsts=[T[m][:, i * w:(i + 1) * w, :]], alu_op=1 if len(srcs) > 1 else 0))
            sent[0] += h
        g.remote_dma_fused(tr, local_sem=T.sem.sent)

    rin = relays_for(prv, core, T, topo)
    arrive = sum(len(topo.engines(c, core)) for c in rin) if rin else len(topo.engines(prv, core))
    for m in MSGS:
        wr[m] = ("ar" + m, arrive)
        total["ar" + m] = arrive

    X, B, GG, ID, ONE, TC, UC, COL, P1 = T.X, T.B, T.GG, T.ID, T.ONE, T.TC, T.UC, T.COL, T.P1
    BN, B0, OF0 = ks("Bn", 4) + ks("Bx", 4), ks("Bo", 4), ks("OF0", 6)

    dma("S", T.RC[:, 0, :], T.rec[0::2, :], w=["RC0"])
    dma("Y", T.RC[:, 1, :], T.rec[1::2, :], w=["RC1"])
    dma("S", T.LR[:, 0, :], T.lc[:], w=["LR0"])
    dma("Y", T.LR[:, 1, :], T.rc[:], w=["LR1"])
    dma("S", T.RTI[:], T.rt[:], w=["RTI"])
    dma("Y", B[:, NV:2 * NV], T.x[:], w=["XR"])
    dma("Y", X[:, NV + 2560:NV + 3072], T.nw[:], w=["Y0"])

    iota(T.PI[:, 0:6], [[0, 6]], 0, 1, flt=False, w=["PI"])
    ms(T.ZT[:], 0.0, w=["ZT"])
    ts(T.PK[:, 0:1], T.PI[:, 0:1], 15, Op.bitwise_and, r=["PI"], w=["PK"])
    ms(ONE[:], 1.0, w=["ONE"])
    ts(COL[:, 0:1], T.PK[:, 0:1], 4.0, Op.is_equal, r=["PK"], w=["COL0"])
    ms(T.SG[:], 1.0, w=["SG"])

    def fill(cs):
        for i in cs:
            act(B[:, i * K:(i + 1) * K], T.ZT[:], bias=COL[:, 0:1], r=["ZT", "COL0"], w=["Bz%d" % i])

    fill(range(6))
    act(B[:, 0:1], T.ZT[:, 0:1], Act.Copy, r=["ZT"], w=["Bz0"])
    iota(T.SV[0:32], [[0, 12], [-1, 6]], -4, w=["SV"])
    iota(T.LAM[0:32], [[0, 2], [1, 6], [0, 6]], -9, w=["LAM"])
    sel(ID[:], ONE[:], [[-1, 128]], Op.is_equal, 0, 1, r=["ONE"], w=["ID"])
    A3, FF = T.A3, T.FF
    ms(T.PJ[0:32, 0::6], 0, w=["PJ0"])
    for i in range(1, 6):
        ts(T.PJ[0:32, i::6], T.PI[0:32, 0:6], 4 if i == 1 else i - 2, Op.logical_shift_right, 1, Op.bitwise_and, r=["PI"], w=["PJ%d" % i])
    ms(T.SG[:, :, 0:2], -1.0, w=["SG"])
    sel(T.WC[:], T.SG[:], [[-16, 8], [0, 8]], Op.is_ge, 0, 1, r=["SG"], w=["WC"])
    sel(T.WC[:], T.WC[:], [[16, 8], [0, 8]], Op.is_ge, 15, -1, w=["WC"])

    def picks(W, key, rows):
        a, b, c, d = rows
        sel(W[:, :, 0:2], ONE[:, :, 0:2], [[-16, 8], [a - b, 2]], Op.is_equal, -a, 1, r=["ONE"], w=[key + "0"])
        sel(W[:, :, 2:4], ONE[:, :, 0:2], [[-16, 8], [c - d, 2]], Op.is_equal, -c, 1, r=["ONE"], w=[key + "1"])
        sel(W[:, :, 4:6], W[:, :, 0:2], [[-16, 8], [c - d, 2]], Op.not_equal, -c, 1, fill=-1.0, r=[key + "0"], w=[key + "2"])
        sel(W[:, :, 6:8], ONE[:, :, 0:2], [[-16, 8], [-1000, 2]], Op.is_equal, -4, 1, r=["ONE"], w=[key + "3"])

    picks(T.WB, "WB", (0, 1, 2, 3))
    iota(UC[0:32, :, :, 0:5], [[0, 180]], 0, w=["UC"])
    for s in range(5):
        iota(UC[0:32, s + 1:6, 0:5 - s, s], [[0, (5 - s) * (5 - s)]], 19200, r=["UC"], w=["UC%d" % s])
    for s in range(4):
        iota(UC[0:32, s + 2:6, 0:4 - s, s], [[0, (4 - s) * (4 - s)]], int(TB) + 512 * (s + 1), w=["UC%d" % s])
    cp(A3[0:32, 36:72], T.PJ[0:32], r=ks("PJ", 6), w=["AH"])
    ts(COL[:, 1:2], T.PK[:, 0:1], 0.5, Op.is_gt, r=["PK"], w=["COL1"])
    for c in (0, 72):
        ts(A3[0:32, c:c + 36], A3[0:32, 36:72], -1.0, Op.mult, 1.0, Op.add, r=["AH"], w=["AL%d" % c])
    ts(COL[:, 5:6], T.PI[:, 0:1], 63.5, Op.is_gt, 256.0, Op.mult, r=["PI"], w=["COL5"])
    ms(A3[0:32, 0::6], 0.0, w=["AH", "AL0", "AL72"])
    ms(T.ZC[:], 0.0, w=["ZC"])
    tt(T.DD[0:32], A3[0:32, 36:108], T.SV[0:32], Op.mult, r=["AH", "AL72", "SV"], w=["DD"])
    ts(COL[:, 2:3], COL[:, 5:6], 2560.0, Op.add, r=["COL5"], w=["COL2"])
    scan(FF[0:32], A3[0:32, 0:72], T.DD[0:32], 0.0, Op.mult, Op.add, r=["AL0", "DD"], w=["FF"])
    ts(COL[:, 3:4], COL[:, 5:6], 2560.0 + 9216, Op.add, r=["COL5"], w=["COL3"])
    tt(T.MK[0:32], T.LAM[0:32], FF[0:32], Op.is_gt, r=["LAM", "FF"], w=["MK"])
    ts(T.VV[0:32], FF[0:32], 512.0, Op.mult, TB + 9 * 512, Op.add, r=["FF"], w=["VV"])
    ms(T.WQ[:], 0.0, w=["WQ"])
    tt(T.MX[0:32, 0:71], T.VV[0:32, 0:71], A3[0:32, 37:108], Op.mult, r=["VV"], w=["MX"])

    def table_hung():
        for d in range(2):
            tt(TC[0:32, :, :, 11 - d], T.MK[0:32, 36 * d:36 * d + 36], T.VV[0:32, 36 * d:36 * d + 36], Op.mult, r=["MK", "VV"], w=["TCm%d" % d])
        for s in range(5):
            for d in range(2):
                c = 36 * d + 4 - s
                ts(TC[0:32, :, 5 - s:6, 2 * s + d], T.LAM[0:32, 0:6, 5 - s:6], FF[0:32, c:c + 1], Op.is_gt, T.MX[0:32, c:c + 1], Op.mult,
                   r=["LAM", "FF", "MX"], w=["TCh%d" % (2 * s + d)])

    def table_unhung():
        for s in range(5):
            for d in range(2):
                c = 36 * (1 + d) + 5 - s
                act(TC[0:32, :, 0:5 - s, 2 * s + d], UC[0:32, :, 0:5 - s, s], scale=A3[0:32, c:c + 1], r=["UC%d" % s, "AH", "AL72"], w=["TCu%d" % (2 * s + d)])

    def table_roots():
        for j in range(2):
            cp(TC[0:32, :, 0:5, 12 + 2 * j:14 + 2 * j], TC[0:32, :, 0:5, 0:2], r=["TCu0", "TCu1"], w=["TCa%d" % (2 * j)])
            cp(TC[0:32, :, 5, 12 + 2 * j:14 + 2 * j], TC[0:32, :, 5, 10:12], r=["TCm0", "TCm1"], w=["TCa%d" % (2 * j + 1)])

    def table_turn(j):
        pn = ("PO", "PL", "PC1")[j]
        mms([(T[pn][0:16, c], TC[0:32, 2 * j + c // 6, c % 6, :], ID[0:32, 0:2, :], True, True) for c in range(12)],
            r=ks("TCh", 10) + ks("TCu", 10) + ks("TCm", 2) + ks("TCa", 4) + ["ID"], pb=[pn])
        act(T.TT[0:16, 384 * j:384 * j + 384], T[pn][0:16, 0:12], Act.Copy, w=["TT%d" % j], pb=[pn])
        if j == 2:
            for q in range(1, 8):
                dma("Y", T.TT[16 * q:16 * q + 16, :], T.TT[0:16, :], r=ks("TT", 3), w=["TR%d" % q])

    for h in range(2):
        cp(T.RF[:, :, h, :], T.RC[:, h, :], r=["RC%d" % h], w=["RF%d" % h])
    ts(T.LR[:, :, 0:1], T.LR[:, :, 0:1], COL[:, 1:2], Op.mult, r=["COL1"], w=["LR0", "LR1"])
    op("V", lambda: V.transpose(T.RT[:], T.RF[:]), r=["RF0", "RF1"], w=["RT"])
    for k in range(6):
        cp(T.OF0[:, k::6], T.RT[:, 32 * k:32 * k + 32], r=["RT"], w=["OF0%d" % k])
    ts(T.FC[:, 0:4:2, :], T.LR[:], 1.0 + 1.0 / 256, Op.mult, r=["LR0", "LR1"], w=["FC0", "FC2"])
    for f in (1, 3):
        tt(T.FC[:, f, :], T.LR[:, f // 2, :], T.FC[:, f - 1, :], Op.subtract, r=["LR0", "LR1", "FC0", "FC2"], w=["FC%d" % f])
    for f in (0, 2, 1, 3):
        dma("Y", B[f::16, 0:NV], T.FC[:, f, :], r=["FC%d" % f] + ks("Bz", 6), w=["Bo%d" % f])

    cp(T.OFA[:], T.RTI[:], r=["RTI"], w=["OFA"])
    ts(T.WP[:], T.WC[:, :, 2:7], 8.0, Op.mult, r=["WC"], w=["WP"])
    cp(X[:, 0:16 * XV], B[:, NV:2 * NV].indirect(T.OF0[:, 0:XV]), r=["XR"] + OF0, w=["XV"])
    act(X[:, 16 * XV:NV], B[:, NV:2 * NV].indirect(T.OF0[:, XV:192]), Act.Copy, r=["XR"] + OF0, w=["XS"])
    ms(X[:, 0:1], 0.0, w=["XV"])
    dma("Y", T.WTI[:, 0:1], T.wt[:], w=["WTI"])

    iota(T.LN[:], [[0, 8], [1, 4]], 0, 4, w=["LN"])
    iota(T.ZR[:], [[0, 288]], 0, w=["ZR0", "ZR1"])
    iota(T.W4[:], [[0, 32], [-1, 4]], 5, w=["W4"])
    iota(T.ZI[:], [[0, 576]], 0, w=ks("ZI", 4))
    iota(T.IDP[:], [[0, 128]], 32, w=["IDP"])
    sel(T.IDP[:], T.IDP[:], [[-1, 128]], Op.is_equal, 0, 1, w=["IDP"])
    if 0 not in FOLD:
        send("LA0", [(X, NV + 2560)], ["Y0"] + B0)
    iota(T.F[:, 6::8, 0::2], [[0, 64]], 0, w=["Fz0"])
    iota(T.F[:, 7::8, 0::2], [[0, 64]], 0, w=["Fz1"])
    iota(T.J0[:], [[0, 4], [1, 128]], 0, w=["J0"])
    sel(T.IDM[:], ID[:], [[0, 8], [-1, 16]], Op.is_ge, 11, 0, r=["ID"], w=["IDM"])
    iota(T.F[:, 5::8, :], [[0, 128]], 0, w=["F5"])
    picks(T.WR, "WR", (12, 14, 13, 15))

    def round1_constants():
        sel(T.SE0[:], ONE[:, :, 0:12], [[-16, 8], [-1, 12]], Op.is_equal, 0, 1, r=["ONE"], w=["SE0"])
        for W, key, c in ((T.SA, "SA", 12), (T.SB, "SB", 14)):
            iota(W[:], [[0, 128]], 0, w=[key])
            sel(W[:, :, c:c + 2], ONE[:, :, 0:2], [[-16, 8], [-1, 2]], Op.is_equal, -10, 1, r=["ONE"], w=[key])

    def round2_constants():
        for W, key in ((T.SE1, "SE1"), (T.SE2, "SE2")):
            sel(W[:, :, 2:12], ONE[:, :, 0:10], [[-16, 8], [-1, 10]], Op.is_equal, 0, 1, r=["ONE"], w=[key])
        iota(T.SE1[:, :, 0:2], [[0, 16]], 0, w=["SE1m"])
        sel(T.SE2[:, :, 0:2], ONE[:, :, 0:2], [[-16, 8], [-1, 2]], Op.is_equal, -12, 1, r=["ONE"], w=["SE2m"])
        sel(T.SE2[:, :, 0:2], T.SE2[:, :, 0:2], [[-16, 8], [-1, 2]], Op.not_equal, -14, 1, fill=1.0, w=["SE2m"])
        for W, key, at, lo in ((T.I12, "I12", 2, True), (T.SM, "SM", -10, False)):
            sel(W[:, 0:24, :], ONE[:, 0:3, :], [[-16, 8], [-1, 6]], Op.is_equal, at, 1, r=["ONE"], w=[key])
            sel(W[:, 0:24, :], W[:, 0:24, :], [[0, 8], [1 if lo else -1, 6]], Op.is_ge, -2 if lo else 1, 0, w=[key])
            iota(W[:, 24:64 - 32 * lo, :], [[0, 80 - 64 * lo]], 0, w=[key + "z"])
        sel(T.I12[:, 32:64, :], ONE[:, 0:4, :], [[-16, 8], [-1, 8]], Op.is_equal, -4, 1, r=["ONE"], w=["I12m"])
        iota(T.F2[:, 24:32, :], [[0, 128]], 0, w=["F2r"])

    def wrap(Z, np_, parts, pn, c0, keys, first=True, final=True, I=ID, ik="ID"):
        lst = [(T[pn][:, c0:c0 + 32], Z[:, 3 - e:35 - e, p::np_], I[:, :, e::4]) for p in parts for e in range(4)]
        mms([a + (first and i == 0, final and i == len(lst) - 1) for i, a in enumerate(lst)], r=keys + [ik], pb=[pn])

    PU = T.PX[:, 64:96]

    def count(A, ak, pn):
        mms([(T[pn][:, 0:8, :, 2 * b:2 * b + 2], A[:, b::4], T.WC[:], True, True) for b in range(4)], r=ak + ["WC"], pb=[pn])

    def sides(lo, hi, pn, klo, khi):
        ts(hi, T[pn][:, 0:8, 1, :], 8.5, Op.is_gt, w=[khi], pb=[pn])
        ts(lo, T[pn][:, 0:8, 0, :], -8.5, Op.is_gt, w=[klo], pb=[pn])

    offs = ["OFA", "OFB"]
    cur = [0]
    ZW = T.ZC[:, 3:35:4, :]
    ZR0, ZR1 = T.ZR[:, 3:35:4, 0::2], T.ZR[:, 3:35:4, 1::2]
    WBK, WRK, HK, AK = ks("WB", 4), ks("WR", 4), ks("HO", 4), ks("A5", 4)

    def zi(p):
        return T.ZI[:, 3:35:4, p::4]

    def records(t):
        return ["XV", "XS"] + ["R%d_%d" % (u, s) for u in range(t) for s in range(6)] + ks("Y", t)

    def look(t, c0, c1):
        Bt = NV + 3072 * t
        tt(T.A5[:, 16 * c0:16 * c1], X[:, 0:Bt].indirect(T.OFC[:, c0:c1]), X[:, Bt + 2560 + 16 * c0:Bt + 2560 + 16 * c1], Op.is_gt,
           r=records(t) + ["OFC", "Y%d" % t], w=AK[c0 // 8:c1 // 8])

    def look_end(pn, where):
        sides(T.G5[:, :, 0:8], T.G5[:, :, 8:16], pn, "G50", "G51")
        if where is None:
            for p in range(2):
                tt(T.F[:, 6 + p::8, 0::2], T.G5[:, :, p::2], T[pn][:, 8:16, 0:2, p::2], Op.mult, r=["G50", "G51"], w=["Fz%d" % p], pb=[pn])
        else:
            tt(where[0], T.G5[:], T[pn][:, 8:16, 0:2, :], Op.mult, r=["G50", "G51"], w=[where[1]], pb=[pn])

    for t in range(3):
        Bt = NV + 3072 * t
        last = t == 2
        yk = "Y%d" % t
        y = X[:, Bt + 2560:Bt + 3072]
        xk = records(t)
        la, lb = "LA%d" % t, "LB%d" % t
        fold = t in FOLD

        def pri(s):
            if s == 0:
                c = Bt + 2560
                lst = []
                for b in range(4):
                    o = T.PX[:, 128 + b:160:4]
                    lst += [(o, X[:, c + b:c + K:4], T.WP[:, :, 0], True, False), (o, X[:, Bt + b:Bt + K:4], T.WM[:], False, True)]
                mms(lst, r=["R%d_0" % t, yk, "WP", "WM"], pb=["PX"])
                return
            if s == 4 and last:
                a, c0, keys = T.A5, 0, AK
            else:
                a, c0, keys = X, Bt + K * s, ["R%d_%d" % (t, s)] + ["R%d_5" % t] * (s == 4)
            mms([(T.PR[:, b::4, s], a[:, c0 + b:c0 + K:4], T.WM[:], False, s == 4 and b == 3) for b in range(4)], r=keys + ["WM"], pb=["PR"])

        def kept(s):
            node = T.F[:, s::8, :] if not last else T.F2[:, 1 + s:24:3, :] if s < 2 else T.F5[:, s - 2::4, :]
            tt(node, GG[:, s], P1[:, 0:8, 0:2, :], Op.mult, r=["GL%d" % s, "GH%d" % s], w=["F%d" % s], pb=["P1"])

        def differ(high, key):
            tt(T.TD[:], high, P1[:, 0:8, 2, :], Op.mult, r=[key], w=["TD"], pb=["P1"])

        def choose():
            tt(ZW, T.TD[:], P1[:, 0:8, 1, :], Op.add, r=["TD"], w=["ZC"], pb=["P1"])

        def root_place():
            if t == 0:
                tt(T.TMP[:], T.U0[:], T.LV[:, 0, :], Op.mult, r=["U0", "LV0"], w=["TMP"])
                ts(ZR0, T.TMP[:], -2560.0 / 192, Op.mult, COL[:, 2:3], Op.add, r=["TMP", "COL2"], w=["ZR0"])
            elif t == 1:
                ts(ZR0, T.U0[:], -2560.0, Op.mult, COL[:, 2:3], Op.add, r=["U0", "COL2"], w=["ZR0"])
            else:
                ts(T.F2[:, 24:32, 0:8:2], T.U0[:], -2560.0, Op.mult, COL[:, 3:4], Op.add, r=["U0", "COL3", "F2r"], w=["F2h"])

        def root_keeps():
            for d in range(2):
                for p in range(2):
                    tt(T.F[:, 6 + p::8, 8 * d + 1:8 * d + 8:2], T.F[:, 0::8, 8 * d + p:8 * d + 8:2], T.U0[:], Op.mult,
                       r=["F0", "U0"], w=["FA%d" % (2 * d + p)])

        lives = T.PX[:, 224:256] if t == 0 else T.PX[:, 192:224]
        jobs = {
            "WM": lambda: ts(T.WM[:], T.WC[:, :, 0], 8.0, Op.mult, r=["WC"], w=["WM"]),
            "over": lambda: ts(COL[:, 6:7], T.PK[:, 0:1], 11.5, Op.is_gt, r=["PK"], w=["COL6"]),
            "under": lambda: ts(T.PK[:, 1:2], T.PK[:, 0:1], 13.5, Op.is_lt, 30720.0, Op.mult, r=["PK"], w=["PK1"]),
            "both": lambda: tt(COL[:, 6:7], COL[:, 6:7], T.PK[:, 1:2], Op.mult, r=["PK1"], w=["COL6"]),
            "LV0": lambda: ts(T.LV[:, 0, :], P1[:, 0:8, 3, 0::2], 192.0, Op.mult, w=["LV0"], pb=["P1"]),
            "ZR1": lambda: ts(ZR1, T.LN[:], COL[:, 5:6], Op.subtract, r=["LN", "COL5"], w=["ZR1"]),
            "LS1": lambda: ts(T.LS[:, :, 1], T.LN[:], COL[:, 5:6], Op.subtract, r=["LN", "COL5"], w=["LS1"]),
            "U0": lambda: ts(T.U0[:], T.PX[:, 128:160], 0.5, Op.is_lt, w=["U0"], pb=["PX"]),
            "T0": lambda: ts(T.T0[:], T.U0[:], -5.0, Op.mult, 6.0, Op.add, r=["U0"], w=["T0"]),
            "hung": table_hung,
            "roots": table_roots,
            "root": root_place,
            "FA": root_keeps,
            "OFC": lambda: cp(T.OFC[:], T.PW[:, 0:32], w=["OFC"], pb=["PW"]),
            "base": lambda: ts(COL[:, 8:9], COL[:, 5:6], float(Bt), Op.add, r=["COL5"], w=["COL8"]),
            "OFR": lambda: cp(T.OFR[:], T.PX[:, 32:64], w=["OFR"], pb=["PX"]),
            "ID2": lambda: ts(T.ID2[:], ID[:], 2.0, Op.mult, r=["ID"], w=["ID2"]),
            "ID4": lambda: ts(T.ID4[:], ID[:], 4.0, Op.mult, r=["ID"], w=["ID4"]),
            "ID8": lambda: ts(T.ID8[:], ID[:], 8.0, Op.mult, r=["ID"], w=["ID8"]),
            "IDN": lambda: ts(T.IDN[:], T.IDP[:], -1.0, Op.mult, r=["IDP"], w=["IDN"]),
            "weight": lambda: cp(COL[:, 4:5], T.WTI[:, 0:1], r=["WTI"], w=["COL4"]),
            "WQ": lambda: ts(T.WQ[:, 15:143:16], T.WP[:, :, 0], COL[:, 4:5], Op.mult, 0.125, Op.mult, r=["WP", "COL4"], w=["WQ"]),
            "LS0": lambda: ts(T.LS[:, :, 0], T.PX[:, 192:224], 8.0 / 3, Op.mult, COL[:, 8:9], Op.add, r=["COL8"], w=["LS0"], pb=["PX"]),
            "RM4": lambda: ts(T.RM4[:], T.W4[:], 4.5, Op.is_lt, r=["W4"], w=["RM4"]),
            "ZI0": lambda: tt(zi(0), GG[:, 3, :, 8:16:2], T.PX[:, 96:128], Op.add, r=["GH3"], w=["ZI0"], pb=["PX"]),
            "ZI1": lambda: tt(zi(1), T.LV[:, 4, :], lives, Op.add, r=["LV4"], w=["ZI1"], pb=["PX"]),
            "F2l": lambda: cp(T.F2[:, 24:32, 1:8:2], T.LS[:, :, 1], r=["LS1", "F2r"], w=["F2l"]),
            "OFD": lambda: ts(T.OFD[:], T.PW[:, 0:32], Bt - 1.0, Op.min, w=["OFD"], pb=["PW"]),
            "ON": lambda: ts(T.ON[:], y, float(t), Op.add, r=[yk], w=["ON"]),
            "J0": lambda: ts(T.J0[:], T.J0[:], COL[:, 6:7], Op.add, r=["COL6"], w=["J0"]),
            "J1": lambda: ts(T.J1[:], T.J0[:], 128.0, Op.add, r=["J0"], w=["J1"]),
            "I12N": lambda: ts(T.I12N[:], T.I12[:], -1.0, Op.mult, r=["I12", "I12m", "I12z"], w=["I12N"]),
            "end": lambda: look_end("PC1", (T.F2[:, 0:24:3, :], "F2m") if last else None),
        }
        for h in range(2):
            jobs["owed%d" % h] = lambda h=h: look(t - 1, 16 * h, 16 * h + 16)

        def early(which):
            mms([(T.PO[0:64, :, :, i // 2::4], T.F2[:, :, i::8], ID[:], False, False) for i in which],
                r=["F0", "F1", "F2m", "F2r", "F2l", "F2h"], pb=["PO"])

        def rows(pn, m, W, key, src, h, first=False, final=False):
            mms([(T[pn][0:m, 8 * h:8 * h + 8], W[:], T[src][:, 256 * h:256 * h + 256], first, final)], r=[src] + key, pb=[pn])

        def owed_out(pn):
            act(T.OUE[0:96, :], T[pn][0:96], Act.Copy, w=["OUE"], pb=[pn])
            c = Bt - 2 * NV - K * last
            for d, o in enumerate((T.yl, T.yr)):
                dma("Y", o[:, c:c + NV], T.OUE[d:96:2, :], r=["OUE"], w=["y%d" % d])

        IK, MK = ["I12", "I12m", "I12z"], ["SM", "SMz"]
        pe = {}
        for h in range(2):
            pe["lo%d" % h] = lambda h=h: rows("PL" if last else "PO", 96, T.SE1 if last else T.SE0, ["SE0", "SE1", "SE1m"], "E1", h, first=h == 0)
            pe["hi%d" % h] = lambda h=h: rows("PL" if last else "PO", 96, T.SE2 if last else T.SE0, ["SE0", "SE2", "SE2m"], "E2", h, final=h == 1)
            pe["a%d" % h] = lambda h=h: rows("PL", 128, T.SA, ["SA"], "E2", h, first=h == 0)
            pe["b%d" % h] = lambda h=h: rows("PL", 128, T.SB, ["SB"], "E1", h)
            pe["m%d" % h] = lambda h=h: rows("PO", 128, T.SM, MK, "E1", h)
            pe["n%d" % h] = lambda h=h: rows("PO", 128, T.SM, MK, "E2", h)
        pe["j"] = lambda: rows("PO", 128, T.I12, IK, "J0", 1, first=True)
        pe["k"] = lambda: mms([(T.PL[:, 0:8], T.IDP[:], T.J0[:, 256:K], True, False)], r=["J0", "IDP"], pb=["PL"])
        pe["out"] = lambda: owed_out("PL")
        for i in range(4):
            pe["e%d" % i] = lambda i=i: early(range(2 * i, 2 * i + 2))

        def side(s, kind):
            for name in SIDE[t].get("%d%s" % (s, kind), "").split():
                pe[name]()

        def gap(s, kind):
            for name in GAPS[t].get("%d%s" % (s, kind), "").split():
                jobs[name]()

        for s in range(5):
            on = offs[cur[0]]
            off = T[on]
            r0 = Bt + K * s
            if s == 0 and t:
                xw, xr, bw, bk, wb, wk = T.XA[:], ["XA"], T.E1[:], ["E1"], T.WR, WRK
            else:
                far = r0 if s == 4 and not last else Bt
                xw, xr = X[:, 0:far], xk + (ks("R%d_" % t, 4) if far > Bt else [])
                bw, bk, wb, wk = B[:, 0:Bt], B0 + BN, T.WB, WBK
            if s == 4 and last:
                tt(T.A5[:], xw.indirect(off[:]), y, Op.subtract, r=xr + [on, yk], w=AK)
                ts(T.A[:], T.A5[:], 0.5, Op.is_gt, r=AK, w=["A"])
            else:
                if s == 4:
                    c = 16 * X4V
                    cp(X[:, r0:r0 + c], xw.indirect(off[:, 0:X4V]), r=xr + [on], w=["R%d_5" % t])
                    act(X[:, r0 + c:r0 + K], xw.indirect(off[:, X4V:32]), Act.Copy, r=xr + [on], w=["R%d_4" % t])
                    more = [(T.ON, 0) if t else (X, Bt + 2560)] if fold else []
                    send(lb, [(X, r0)] + more, ["R%d_4" % t, "R%d_5" % t, yk] + ["ON"] * t)
                    (round1_constants, round2_constants)[t]()
                tt(T.A[:], xw.indirect(off[:]), y, Op.is_gt, r=xr + [on, yk], w=["A"])
            bn = "OFD" if s == 4 and not last else on
            act(T.BT[:], bw.indirect(T[bn][:]), Act.Copy, r=bk + [bn], w=["BT"])
            if s < 4:
                act(X[:, r0:r0 + K], xw.indirect(off[:]), Act.Copy, r=xr + [on], w=["R%d_%d" % (t, s)])

            if t == 0 and s == 0:
                table_unhung()

            def children():
                mms([(P1[:, 0:8, :, 2 * b:2 * b + 2], T.BT[:, b::4], wb[:], True, True) for b in range(4)], r=["BT"] + wk, pb=["P1"])

            if s:
                pri(s - 1)
            else:
                c, nc = Bt + 2560, 5 - last
                mms([(T.PR[:, b::4, 1:nc], X[:, c + b:c + K:4], T.WP[:, :, 1:nc], b == 0, False) for b in range(4)], r=[yk, "WP"], pb=["PR"])
            if s < 4:
                side(s, "w")
            if t == 0 and s in (1, 2):
                for j in range(2 * s - 2, s + 1):
                    table_turn(j)
            if t and s == LOOK[t]:
                count(T.A5, AK, "PC1")
            if s == 3:
                lst = [(T.PX[:, 96:128], T["ID%d" % (8 >> u)][:], GG[:, u, :, 8:16:2], u == 0, u == 2) for u in range(3)]
                lst += [(T.PX[:, 192:224], ID[:], T.LV[:, u, :], u == 1, u == 3) for u in range(1, 4)]
                if t == 0:
                    lst += [(lives, ID[:], T.LV[:, u, :], u == 0, u == 3) for u in range(4)]
                mms(lst, r=ks("GH", 3) + ks("LV", 4) + ["ID2", "ID4", "ID8"], pb=["PX"])
            if s == 4:
                break
            count(T.A, ["A"], "PC0")
            children()
            gap(s, "c")
            if t == 1 and s == 0:
                if not fold:
                    send(la, [(T.ON, 0)], ["ON"])
                for i in (2, 3, 4, 5, 0, 1):
                    iota(B[:, Bt + K * i:Bt + K * (i + 1)], [[0, K]], 0, r=BN if i < 2 else [], w=["Bf%d" % i])
            side(s, "m")
            sides(GG[:, s, :, 0:8], GG[:, s, :, 8:16], "PC0", "GL%d" % s, "GH%d" % s)
            differ(GG[:, s, :, 8:16], "GH%d" % s)
            choose()
            idle = s == 3 and not last
            wrap(T.ZC, 2, (0, 1), "PW", 0, ["ZC"], final=not idle)
            if idle:
                kept(s)
                for p in range(2):
                    ts(T.E4[:, :, p], T.ZC[:, 3:35:4, 0::2], 0.5, Op.is_lt, r=["ZC"], w=["E4%d" % p])
                ts(T.LV[:, 4, :], T.ZC[:, 3:35:4, 0::2], 0.5, Op.is_gt, 192.0, Op.mult, r=["ZC"], w=["LV4"])
                tt(T.ZR[:, 3:35:4, :], T.E4[:], T.LS[:], Op.mult, r=["E40", "E41", "LS0", "LS1"], w=["ZR0", "ZR1"])
                wrap(T.ZR, 2, (0, 1), "PW", 0, ["ZR0", "ZR1"], first=False)
            else:
                kept(s)
                ts(T.LV[:, s + 1, :], T.ZC[:, 3:35:4, 0::2], 0.5, Op.is_gt, 192.0, Op.mult, r=["ZC"], w=["LV%d" % (s + 1)])
            gap(s, "w")
            cur[0] ^= 1
            cp(T[offs[cur[0]]][:], T.PW[:, 0:32], w=[offs[cur[0]]], pb=["PW"])
            gap(s, "e")
            if s == 1 and not last:
                wrap(T.ZR, 2, (0, 1), "PX", 32, ["ZR0", "ZR1"])

        wrap(T.ZI, 4, (0, 1), "PX", 0, ["ZI0", "ZI1"], final=False)
        side(4, "w")
        pri(4)
        if last:
            children()
        count(T.A, ["A"], "PC0")
        if not last:
            children()
        tt(T.LT[:], T.PR[:, :, 1:5], T.W4[:], Op.min, r=["W4"], w=["LT"], pb=["PR"])
        scan(T.NH[:], T.RM4[:], T.LT[:], 0.0, Op.mult, Op.max, r=["RM4", "LT"], w=["NH"])
        if last:
            sides(T.N4[:], T.H4[:], "PC0", "N4", "H4")
        ts(zi(2), T.PC0[:, 0:8, 1, 0::2], 8.5, Op.is_gt, 16.0, Op.mult, w=["ZI2"], pb=["PC0"])
        if last:
            differ(T.H4[:], "H4")
        wrap(T.ZI, 4, (2,), "PX", 0, ["ZI2"], first=False, final=False)
        tt(zi(3), T.NH[:, 3::4], T.T0[:], Op.max, r=["NH", "T0"], w=["ZI3"])
        wrap(T.ZI, 4, (3,), "PX", 0, ["ZI3"], first=False, I=T.IDP, ik="IDP")
        if last:
            choose()
            wrap(T.ZC, 2, (0, 1), "PW", 0, ["ZC"])
        else:
            sides(T.N4[:], T.H4[:], "PC0", "N4", "H4")
        if t == 1:
            owed_out("PO")
        for p in range(2):
            tt(T.Q4[:, :, p], zi(3), T.LV[:, 4, :], Op.min, r=["ZI3", "LV4"], w=["Q4%d" % p])
        tt(GG[:, 4, :, 0:8], T.Q4[:], T.H4[:], Op.is_gt, r=["Q40", "Q41", "H4"], w=["GL4"])
        tt(GG[:, 4, :, 8:16], T.Q4[:], T.N4[:], Op.is_gt, r=["Q40", "Q41", "N4"], w=["GH4"])
        ts(T.Q5[:], T.Q4[:], 1.0, Op.is_equal, r=["Q40", "Q41"], w=["Q5"])
        if not last:
            kept(4)
        ts(T.OFI[:], T.PX[:, 0:32], 160.0 if t else -32.0, Op.add, w=["OFI"], pb=["PX"])
        if not last:
            differ(T.H4[:], "H4")
        for q in (2, 3, 0, 1):
            a = (T.HO[:, 128 * q:128 * q + 128], T.TT[:].indirect(T.OFI[:, 8 * q:8 * q + 8]))
            bias, kw = Bt + 128.0 * (q - (t == 1)) - TB, dict(r=ks("TT", 3) + ks("TR", 8) + ["OFI"], w=["HO%d" % q])
            if last or q >= 2:
                act(*a, Act.Relu, bias=bias, **kw)
            else:
                ts(*a, bias, Op.add, 0.0, Op.max, **kw)
        if not last:
            choose()
        tt(T.CM[:], ZW, T.Q5[:], Op.mult, r=["ZC", "Q5"], w=["CM"])
        fk = ks("F", 6) + ["ID"]

        def last_child(pn):
            mms([(T[pn][:, 8:16, d, :], ID[:], T.CM[:], True, True) for d in range(2)], r=["CM", "ID"], pb=[pn])

        if last:
            lo, hi = slice(0, 256), slice(256, K)
            jobs["OFC"]()
            look(t, 0, 32)
            kept(4)
            last_child("PC1")
            mms([(T.PL[:, 0:8], T.IDN[:], T.HO[:, hi], False, True), (T.PO[:, 8:16], T.I12[:], T.HO[:, hi], False, False)],
                r=HK[2:4] + ["IDN"], pb=["PL", "PO"])
            act(T.LO[:, hi], T.PL[:, 0:8], Act.Relu, scale=1.0 / 32, w=["LO1"], pb=["PL"])
            mms([(T.PO[:, 0:8], T.I12[:], T.HO[:, lo], False, False)], r=HK, pb=["PO"])
            tt(T.LO[:, lo], T.HO[:, lo], T.J0[:, lo], Op.min, r=HK[0:2] + ["J0"], w=["LO0"])
            count(T.A5, AK, "PC1")
            mms([(T.PO[:, 8:16], T.I12N[:], T.LO[:, hi], False, False)], r=["LO1", "I12N"], pb=["PO"])
            mms([(T.PO[:, 0:8], T.I12[:], T.LO[:, lo], False, True)], r=["LO0"], pb=["PO"])
            act(T.OUT[:], T.PO[:], Act.Copy, w=["OUT"], pb=["PO"])
            dma("S", T.yl[:, Bt - NV - K:Bt - NV + 2 * K], T.OUT[0:48:2, :], r=["OUT"], w=["y0"])
            dma("Y", T.yr[:, Bt - NV - K:Bt - NV + 2 * K], T.OUT[1:48:2, :], r=["OUT"], w=["y1"])
            dma("Y", T.yt[:], T.OUT[48:64:2, :], r=["OUT"])
            look_end("PC1", (T.F5[:, 3::4, :], "F5"))
            mms([(T.PR[64:128, 0:16, i // 2::4], T.F5[:, :, i::8], ID[:, 0:4, :], i % 2 == 0, i % 2 == 1) for i in range(8)], r=fk, pb=["PR"])
            mms([(T.PX[64:128, i // 2:256:4], T.F5[:, :, i::8], ID[:, 4:8, :], i % 2 == 0, i % 2 == 1) for i in range(8)], r=fk, pb=["PX"])
            tt(T.OUM[64:128, lo], T.PR[64:128, 0:16, :], T.OUT[64:128, lo], Op.add, r=["OUT"], w=["OUM0"], pb=["PR"])
            tt(T.OUM[64:128, hi], T.PX[64:128, 0:256], T.OUT[64:128, hi], Op.add, r=["OUT"], w=["OUM1"], pb=["PX"])
            dma("S", T.yl[:, Bt - 4 * K:Bt], T.OUM[64::2, :], r=["OUM0", "OUM1"])
            dma("Y", T.yr[:, Bt - 4 * K:Bt], T.OUM[65::2, :], r=["OUM0", "OUM1"])
            break

        def parts(nm, part, first):
            mms([(T[nm][:, :, :, b::4], T.F[:, :, 2 * b + part::8], ID[:], first and b == 0, not first and b == 3) for b in range(4)],
                r=fk + ks("FA", 4) + ["Fz0", "Fz1"], pb=[nm])

        act(T.XA[:], X[:, Bt:Bt + 3072].indirect(T.OFR[:]), Act.Copy, r=ks("R%d_" % t, 6) + [yk, "OFR"], w=["XA"])
        parts("PO", 1, True)
        for q in (0, 2, 1, 3):
            mms([(T.PO[:, 4 * q:4 * q + 4], ID[:], T.HO[:, 128 * q:128 * q + 128], False, q == 3)], r=["HO%d" % q], pb=["PO"])
        mms([(T.PL[:], T.IDM[:], T.HO[:], t == 0, False)], r=HK + ["IDM"], pb=["PL"])
        parts("PL", 0, False)
        jn = "J%d" % t
        gap(4, "a")
        tt(T.E1[:], T.PO[:], T[jn][:], Op.min, r=[jn], w=["E1"], pb=["PO"])
        act(T.E2[:], T.PL[:], Act.Copy, w=["E2"], pb=["PL"])
        for part, nm in ((1, "E1"), (0, "E2")):
            for side in range(2):
                dma("Y", B[2 * side + part::16, Bt:Bt + 4096], T[nm][side::2, :], r=[nm, "XV", "XS"] + ks("Bf", 6), w=["Bn%d" % (2 * side + part)])
        if t:
            for k, f in enumerate((0, 2, 1, 3)):
                dma("Y", B[f::16, Bt - K:Bt], T.E2[12 + k::16, :], r=["E2"], w=["Bx%d" % k])

        n0 = Bt + 3072 + 2560
        ss, nk = (T[lb] if fold else T.SS), "Y%d" % (t + 1)

        def weigh(src, rs, keys, first=False, final=False):
            mms([(PU, T.WQ[:, 15 - r:143 - r], src[:, :, r], first and r == 0, final and r == 15) for r in rs], r=["WQ"] + keys, pb=["PX"])

        if not fold:
            weigh(T[la], range(16), [la], first=True)
        wrap(T.ZC, 2, (0, 1), "PW", 0, ["ZC"])
        last_child("PC1")
        weigh(T[lb], range(16), [lb], first=fold)
        for h in range(2):
            if not fold:
                tt(T.SS[:, :, h::2], T[la][:, :, h::2], T[lb][:, :, h::2], Op.add, r=[la, lb], w=["SS%d" % h])
        for h in range(2):
            ts(T.MM[:, :, h::2], ss[:, :, h::2], 15.5, Op.is_gt, -16.0, Op.mult, r=["SS%d" % h, lb], w=["MM%d" % h])
            weigh(T.MM, range(h, 16, 2), ["MM%d" % h], final=True)
        tt(X[:, n0:n0 + K], ss[:], T.MM[:], Op.add, r=["SS0", "SS1", "MM0", "MM1"], w=[nk])
        cp(T.UI[:], PU, w=["UI"], pb=["PX"])
        ts(T.UJ[:], T.UI[:], K - 1, Op.bitwise_and, r=["UI"], w=["UJ"])
        cur[0] ^= 1
        cp(T[offs[cur[0]]][:], T.UJ[:], r=["UJ"], w=[offs[cur[0]]])

    total["sent"] = sent[0]
    wait("G", list(total.items()))
